import numpy as np, ml_dtypes
CORES = [242,247,114,119]
N = 4
BF = ml_dtypes.bfloat16
W, L, P, ST, IP = 2048, 128, 32, 5, 0.03125
def probes(s, w):
    u = np.sum(w[:, :, 0:1] * s, axis=1); v = 2 * (np.sum(w[:, :, 1:2] * s, axis=1) & (W // 2 - 1)) + 1
    return (u[:, None, :] + np.arange(P)[None, :, None] * v[:, None, :]) & (W - 1)
def margins(rng, share):
    k = (N, 8, 1, W)
    return np.where(rng.random(k) < share, 0.03 * rng.random(k), 0.1 + 0.4 * rng.random(k))
def sizes(rng):
    return rng.choice(np.array([0, 2, 6, 20]), (N, 8, 1, W))
def rules(rng, z, m):
    h = (N, 8, 16, W); m = m.astype(np.float32); z = np.minimum(z, 0.5).astype(np.float32)
    e = (np.minimum(np.floor((2 * m + 1) * rng.random(h, dtype=np.float32)), 2 * m) - m).astype(np.int32)
    a = np.maximum(0, -e); b = 255 - np.maximum(0, e)
    lo = a + np.floor(z * rng.random(h, dtype=np.float32) * (b - a)).astype(np.int32)
    hi = b - np.floor(z * rng.random(h, dtype=np.float32) * (b - a)).astype(np.int32)
    return lo, hi, e
def start(rng):
    s = rng.integers(0, 256, (N, 8, 16, L)); s = np.where(rng.random((N, 8, 1, L)) < 0.5, s, 64 + s // 2)
    return s, rng.integers(0, 2048, (N, 8, 16, 2)), rng.integers(0, 256, (N, 8, 16, ST)) >> rng.integers(0, 4, (N, 8, 16, ST))
def put(lo, hi, e, q, g, c, a, b, f):
    c, k = np.unique(c, return_index=True)
    lo[q, g][:, c] = a[:, k]; hi[q, g][:, c] = b[:, k]; e[q, g][:, c] = f[:, k]
def pack(lo, hi, e, s, w, d):
    t = lambda x: np.ascontiguousarray(x.reshape(N, 128, -1)).astype(np.float32).astype(BF)
    return {"lo": t(lo), "hi": t(hi), "ef": t(e), "s0": t(s), "wt": np.ascontiguousarray(w.reshape(N, 128, 2)).astype(np.int32), "dr": t(d)}
def setup_inputs(rng):
    share = rng.choice(np.array([1.5, 2.5, 4.0, 6.0]), (N, 8, 1, 1)) * IP
    return pack(*rules(rng, margins(rng, share), sizes(rng)), *start(rng))
def setup_inputs_alike(rng):
    z = margins(rng, 3 * IP); z[:, ::2] = 0.1
    lo, hi, e = rules(rng, z, sizes(rng)); s, w, d = start(rng)
    w[:, 0] = 0; w[:, 4] = 0; w[:, 2] = 0; w[:, 2, 0, 0] = 1; w[:, 6] = 0; w[:, 6, 15, 1] = W // 2 - 1; s[:, 6, 15] = 1
    k = rng.integers(0, 5, (N, 4, 1, L)); s[:, 1::2] = np.take_along_axis(s[:, 1::2, :, :5], k, 3)
    s[:, 5] = 255; s[:, 5, 15] = 255 - rng.integers(0, 4, (N, L)); s[:, 5, 15, :4] = 255 - np.arange(4)
    w[:, 5, :, 0] = 2047; w[:, 5, :, 1] = 0; w[:, 5, 0, 1] = 257
    x = np.full((8, 16, 4), 255); x[:, 15] = 255 - np.arange(4); b = x[5]
    for q in range(N):
        c = probes(x, w[q])[5]; a = rng.integers(0, 200, (16, 4 * P))
        put(lo, hi, e, q, 5, c.reshape(-1), a, a, 0 * a)
        a = b - rng.integers(0, 10, (16, 4)); a[15] = b[15]
        m = np.zeros((16, 4), np.int64); m[15] = np.arange(4) - rng.permutation(4)
        put(lo, hi, e, q, 5, c[P - 1], a, b, m)
    return pack(lo, hi, e, s, w, d)
def setup_inputs_chains(rng):
    lo, hi, e = rules(rng, margins(rng, 0.5 * IP), sizes(rng)); s, w, d = start(rng)
    s[:, ::2] = rng.choice(np.array([0, 1, 254, 255]), (N, 4, 16, L)); s[:, 2:4, :, 0] = 0
    for q in range(N):
        c = probes(s[q], w[q]); k = rng.choice(np.array([0, 1, 2, P // 2, P - 1]), (8, L)); k[2:4, 0] = 2
        for g in range(8): put(lo, hi, e, q, g, c[g, k[g], np.arange(L)], s[q, g], s[q, g], s[(q + 1) % N, g] - s[q, g])
    lo[:, 2:4, :, :2] = 1; hi[:, 2:4, :, :2] = 1; e[:, 2:4, :, :2] = 0
    d[:, 0] = 0; d[:, 1] = 255
    return pack(lo, hi, e, s, w, d)
def setup_inputs_full(rng):
    lo = rng.integers(0, 256, (N, 8, 16, W)); hi = lo.copy(); e = rng.integers(0, 256, (N, 8, 16, W)) - lo
    s, w, d = start(rng); s = rng.integers(100, 156, (N, 8, 16, L)); w = np.zeros((N, 8, 16, 2), np.int64); M = W // L; j = np.arange(L)
    for g in range(8):
        val = np.concatenate([rng.permutation(255)[:L - 1], np.array([255])]) if g % 2 == 0 else np.arange(L)
        for q in range(N):
            s[q, g, 0] = rng.permutation(val)
            if g % 2 == 0:
                s[q, g, 1] = 2; w[q, g, 0, 0] = 1; w[q, g, 1, 0] = 128 * (rng.integers(0, W // 256) if g < 6 else W // 256 - 1)
                k = np.full(L, rng.integers(0, 2))
            else:
                s[q, g, 1] = 1; w[q, g, 0, 0] = M; w[q, g, 1, 0] = rng.integers(0, M) if g < 7 else M - 1
                k = rng.integers(0, 2, L)
            w[q, g, 1, 1] = rng.integers(0, 2048)
            c = probes(s[q], w[q])[g]
            a = rng.integers(10, 65, (16, L)); b = rng.integers(191, 246, (16, L)); m = rng.integers(-9, 10, (16, L)); m[15] = rng.integers(1, 10, L)
            a[0] = s[q, g, 0]; b[0] = s[q, g, 0]; m[0] = rng.permutation(val) - s[q, g, 0]; a[1] = 0; b[1] = 255; m[1] = 0
            put(lo, hi, e, q, g, c[k, j], a, b, m)
    return pack(lo, hi, e, s, w, d)
def setup_inputs_ties(rng):
    lo, hi, e = rules(rng, margins(rng, 2.5 * IP), sizes(rng)); s, w, d = start(rng)
    for q in range(N):
        c = probes(s[q], w[q]); o = rng.permutation(8)
        for g in o[:2]:
            lo[q, g] = rng.integers(0, 256, (16, W)); hi[q, g] = lo[q, g]; e[q, g] = rng.integers(0, 256, (16, W)) - lo[q, g]
        for g in o[2:4]:
            lo[q, g] = 0; hi[q, g] = 255; e[q, g] = 0
        for g in o[4:]:
            x = s[q, g]; mode = rng.integers(0, 4, (1, L)); k = rng.integers(0, 3, L)
            one = (np.arange(16)[:, None] == rng.integers(0, 16, (1, L))) & (mode == 1)
            y = np.where(one, x + np.where(x < 128, 1, -1), x)
            a = np.where(mode == 3, np.floor(x * rng.random((16, L))).astype(np.int64), y)
            b = np.where(mode == 2, x + np.floor((255 - x) * rng.random((16, L))).astype(np.int64), y)
            put(lo, hi, e, q, g, c[g, k, np.arange(L)], a, b, np.minimum(np.maximum(rng.integers(-9, 10, (16, L)), -a), 255 - b))
    return pack(lo, hi, e, s, w, d)
def setup_inputs_spread(rng):
    k = (N, 8, 1, W)
    z = np.where(rng.random(k) < 6 * IP, np.exp2(-1 - 9 * rng.random(k)), 0.5)
    lo, hi, e = rules(rng, z, np.floor(np.exp2(8 * rng.random(k))) - 1); s, w, d = start(rng)
    s = np.floor(rng.random((N, 8, 16, L)) * np.exp2(rng.integers(0, 9, (N, 8, 1, L)))).astype(np.int64)
    s = np.where(rng.random((N, 8, 16, L)) < 0.3, 255 - s, s)
    w = np.floor(rng.random((N, 8, 16, 2)) * np.exp2(rng.integers(1, 12, (N, 8, 16, 2)))).astype(np.int64)
    d = np.floor(rng.random((N, 8, 16, ST)) * np.exp2(rng.integers(0, 9, (N, 8, 16, ST)))).astype(np.int64)
    return pack(lo, hi, e, s, w, d)
def check_inputs(d):
    bad = []; v = {k: np.asarray(d[k]).astype(np.float32) for k in ("lo", "hi", "ef", "s0", "dr")}
    for k in v:
        if not np.all(v[k] == np.floor(v[k])): bad.append("whole numbers in " + k)
    if not np.all((v["lo"] >= 0) & (v["lo"] <= v["hi"]) & (v["hi"] <= 255)): bad.append("0 <= lo <= hi <= 255")
    if not np.all((v["lo"] + v["ef"] >= 0) & (v["hi"] + v["ef"] <= 255)): bad.append("lo + ef >= 0 and hi + ef <= 255")
    for k in ("s0", "dr"):
        if not np.all((v[k] >= 0) & (v[k] <= 255)): bad.append("range of " + k)
    if not np.all((d["wt"] >= 0) & (d["wt"] <= 2047)): bad.append("range of wt")
    return bad
def reference(lo, hi, ef, s0, wt, dr):
    tl, th, te, s, d = [x.astype(np.float32).astype(np.int64).reshape(N, 8, 16, -1) for x in (lo, hi, ef, s0, dr)]
    w = wt.astype(np.int64).reshape(N, 8, 16, 2); st = [s[r] for r in range(N)]; y = np.zeros((N, 8, ST, L), np.int64); old = []
    for t in range(ST):
        now = []
        for r in range(N):
            x = st[r]; c = probes(x, w[r]); ix = c.reshape(8, 1, P * L)
            a = np.take_along_axis(tl[r], ix, 2).reshape(8, 16, P, L); b = np.take_along_axis(th[r], ix, 2).reshape(8, 16, P, L)
            ok = np.all((a <= x[:, :, None, :]) & (x[:, :, None, :] <= b), axis=1)
            fired = np.any(ok, axis=1); i = np.argmax(ok, axis=1)
            col = np.take_along_axis(c, i[:, None, :], 1); place = np.take_along_axis(c, np.maximum(i - 1, 0)[:, None, :], 1)[:, 0]
            fl, fh, fe = [np.take_along_axis(v[r], col, 2) for v in (tl, th, te)]
            y[r, :, t] = np.where(fired, i, P)
            st[r] = np.where(fired[:, None, :], x + fe, np.abs(x - d[r, :, :, t:t + 1]))
            now.append((fired, fl, fh, fe, place))
        if t > 0:
            for r in range(N):
                f0, l0, h0, e0, p0 = old[r]; f1, l1, h1, e1, p1 = now[(r + 1) % N]
                cl = np.maximum(l0, l1 - e0); ch = np.minimum(h0, h1 - e0); ce = e0 + e1
                for g in range(8):
                    m = np.flatnonzero(f0[g] & f1[g]); cols, first = np.unique(p0[g][m], return_index=True); k = m[first]
                    tl[r, g][:, cols] = cl[g][:, k]; th[r, g][:, cols] = ch[g][:, k]; te[r, g][:, cols] = ce[g][:, k]
        old = now
        if t < ST - 1: st = [st[(r - 1) % N] for r in range(N)]
    return {"ys": np.stack(st).reshape(N, 128, L).astype(np.float32), "yp": y.reshape(N, 8, ST * L).astype(np.float32)}

@@ -1,0 +1,447 @@
+from concourse.mybir import AluOpType as Op, ActivationFunctionType as Act
+
+W, L, ST = 2048, 128, 5
+OWN, SPARE, TW = 2048, 2176, 2304
+C = 1024.5 - 1.0 / 2048
+BIG = float(2 ** 19)
+EW = [128 - 16 * a for a in range(8)]
+EO = [sum(EW[:a]) for a in range(8)]
+EN = sum(EW)
+F32, BF, F16, I32, U16 = "float32", "bfloat16", "float16", "int32", "uint16"
+SCRATCH = {}
+for _d, _names in (
+        (F32, dict(A=TW, WF=2, D2=8, ND=8, WG=32, PC=4, COL=144, COLG=128, COLL=128, COLK=192, K2=32, KTAB=256, KT=64, L16=8,
+                   LNP=8, DUM=8, MG=8, NM=16, RST=128, RK=192, I4=128, BLK=128, B=1024, KEY=256, ZK=256, ZL=64, R2=16, R1=8, KR=8,
+                   G=128, FS=8, Z=128, VD=8, FL=8, M1=8, FA=24, T1=8, NK=8, DD=8, D=24, PD=128, TA=EN, O1=8, O2=8, AC=128,
+                   YS=128, YP=640)),
+        (BF, dict(LO=TW, EF=TW, HI=W, DR=8, KC1=256, KC2=256, ONE=128, CB=32, CM=128, ID=128, NI=128, IK=128, IS=128, NS=128,
+                  NBLK=128, BIGM=144, RR=128, LG=4096, SC=EN, FB3=128, SP=128)),
+        (F16, dict(WH=32, PHI=4096)),
+        (I32, dict(WT=2, WI=32, WJ=32, PI=4, X0=256, XI=256, KI=8, CK=16, P1=8, PL=24)),
+        (U16, dict(XU=256, CU=16, OU=8))):
+    for _k, _n in _names.items():
+        SCRATCH[_k] = ("sbuf", [128, _n], _d)
+SCRATCH["SM"] = ("sbuf", [128, 8, 8, 16], BF)
+for _k, _s in dict(pX=[8, 8, 8], pE=[8, 8, 8], pF=[8, 8, 8], pN=[4, 8, 16], pK=[4, 8, 16], pP=[512], pC=[512], pA=[512]).items():
+    SCRATCH[_k] = ("psum", [128] + _s, F32)
+for _k, _ts, _n in (("S", range(5), 128),
+                    ("SO", range(4), 128),
+                    ("FB", range(3), 384 + EN),
+                    ("AL", range(3), 384 + EN),
+                    ("MS", range(1, 4), 264),
+                    ("BL", range(1, 4), 264),
+                    ("ME", range(1, 4), 128),
+                    ("BE", range(1, 4), 128)):
+    for _t in _ts:
+        SCRATCH["%s%d" % (_k, _t)] = ("sbuf", [128, _n], BF)
+
+SEMAPHORES = (["qg", "qv", "qs", "qp", "sent", "d_s0", "d_wt", "d_dr", "d_ef", "d_ys", "d_yp0", "d_yp1", "r_p"]
+              + ["d_lo%d" % k for k in range(4)] + ["d_hi%d" % k for k in range(4)]
+              + ["r_s%d" % t for t in range(1, 5)] + ["r_a%d" % t for t in range(3)] + ["r_q%d" % t for t in range(3)]
+              + ["r_b%d" % t for t in range(1, 4)] + ["r_e%d" % t for t in range(1, 4)])
+
+
+def _engines(topo, cores, r, kind, t):
+    n = len(cores)
+    fwd, back = topo.mask(cores[r % n], cores[(r + 1) % n]), topo.mask(cores[r % n], cores[(r - 1) % n])
+    if kind in "psaq":
+        return fwd
+    return fwd & back if (kind, t) == ("b", 1) else back
+
+
+def rank_program(g, core, T, topo):
+    rank = T.rank_of(core)
+    if rank is None:
+        return
+    n = len(T.cores)
+    nxt, prv = T.cores[(rank + 1) % n], T.cores[(rank - 1) % n]
+
+    Q = {"g": g, "v": g.vector, "s": g.scalar, "p": g.tensor, "y": g.sync}
+    seen = {q: {} for q in Q}
+    total, clock, wrote, read = {}, {}, {}, {}
+
+    def wait(q, toks):
+        best = {}
+        for s, v in toks:
+            if not (q == "p" and s == "qp"):
+                best[s] = max(best.get(s, 0), v)
+        for s, v in sorted(best.items(), key=lambda e: -len(clock.get(e, {}))):
+            if seen[q].get(s, 0) < v:
+                Q[q].wait_ge(T.sem[s], v)
+                seen[q][s] = v
+                for s2, v2 in clock.get((s, v), {}).items():
+                    if seen[q].get(s2, 0) < v2:
+                        seen[q][s2] = v2
+
+    def op(q, fn, r, w, sem=None, inc=1):
+        toks = []
+        for x in r:
+            toks += wrote.get(x, [])
+            if x[0] == "p":
+                toks += [k for k in read.get(x, []) if k[0] != "q" + q]
+        for x in w:
+            toks += wrote.get(x, []) + read.get(x, [])
+        wait(q, toks)
+        s = sem or "q" + q
+        fn().then_inc(T.sem[s], inc)
+        total[s] = total.get(s, 0) + inc
+        tok = (s, total[s])
+        clock[tok] = dict(seen[q])
+        for x in r:
+            read.setdefault(x, []).append(tok)
+        for x in w:
+            wrote[x], read[x] = [tok], []
+
+    def dma(q, out, in_, r, w, sem):
+        op(q, lambda: Q[q].dma_start(out, in_), r, w, sem, 16)
+
+    def send(dst, kind, t, out, in_, r, sem):
+        mask = _engines(topo, T.cores, rank, kind, t)
+        wait("g", [k for x in r for k in wrote.get(x, [])])
+        rid, pid = topo.addr(dst, core)
+        g.remote_dma(out, in_, T.sem[sem], T.sem["sent"], pid, rid, mask)
+        total["sent"] = total.get("sent", 0) + bin(mask).count("1")
+
+    def lands(x, sem, r, kind, t):
+        k = bin(_engines(topo, T.cores, r, kind, t)).count("1")
+        wrote[x], total[sem] = [(sem, k)], k
+
+    V, S, P = g.vector, g.scalar, g.tensor
+
+    def ts(out, in0, s1, s2, o0, o1, r, w):
+        if o1 is None:
+            op("v", lambda: V.tensor_scalar(out, in0, s1, None, o0), r, w)
+        else:
+            op("v", lambda: V.tensor_scalar(out, in0, s1, s2, o0, o1), r, w)
+
+    def tt(out, a, b, o, r, w):
+        op("v", lambda: V.tensor_tensor(out, a, b, o), r, w)
+
+    def cp(out, a, r, w):
+        op("v", lambda: V.tensor_copy(out, a), r, w)
+
+    def ms(out, c, w):
+        op("v", lambda: V.memset(out, c), [], w)
+
+    def scan(out, d0, d1, r, w):
+        op("v", lambda: V.tensor_tensor_scan(out, d0, d1, 0.0, Op.min, Op.max), r, w)
+
+    def act(out, a, f, r, w, bias=0.0, scale=1.0):
+        op("s", lambda: S.activation(out, a, f, bias=bias, scale=scale), r, w)
+
+    def mm(out, lt, rh, st, sp, r, w):
+        op("p", lambda: P.matmul(out, lt, rh, st, sp), r, w)
+
+    def iota(out, pat, base, cm, w, whole=False):
+        if whole:
+            op("g", lambda: g.iota(out, pat, base, cm), [], w)
+        else:
+            op("g", lambda: g.iota(out, pat, base, cm, allow_small_or_imprecise_dtypes=True), [], w)
+
+    lands("SP", "r_p", rank - 1, "p", 0)
+    for t in range(4):
+        lands("S%d" % (t + 1), "r_s%d" % (t + 1), rank - 1, "s", t)
+    for t in range(3):
+        lands("AL%d" % t, "r_a%d" % t, rank - 1, "a", t)
+        lands("AQ%d" % t, "r_q%d" % t, rank - 1, "q", t)
+        lands("BL%d" % (t + 1), "r_b%d" % (t + 1), rank + 1, "b", t + 1)
+        lands("BE%d" % (t + 1), "r_e%d" % (t + 1), rank + 1, "e", t + 1)
+
+    dma("y", T.S0[:], T.s0[:], [], ["S0"], "d_s0")
+    dma("s", T.WT[:], T.wt[:], [], ["WT"], "d_wt")
+    for h in range(4):
+        cs = slice(512 * h, 512 * h + 512)
+        dma("y", T.LO[:, cs], T.lo[:, cs], [], ["LO%d" % h], "d_lo%d" % h)
+        dma("s", T.HI[:, cs], T.hi[:, cs], [], ["HI%d" % h], "d_hi%d" % h)
+    dma("y", T.DR[:, 0:ST], T.dr[:], ["HI3"], ["DR"], "d_dr")
+    dma("y", T.EF[:, 0:W], T.ef[:], ["HI3"], ["EF"], "d_ef")
+
+    iota(T.PI[:, 0:1], [[0, 1]], 0, 1, ["PI0"], True)
+    iota(T.COL[:], [[1, 144]], 0, 0, ["COL"])
+    iota(T.K2[:], [[2, 32]], 0, 0, ["K2"])
+    iota(T.KTAB[:], [[8, 4], [0, 8], [1, 8]], 0, 0, ["KTAB"])
+    iota(T.L16[:], [[16, 8]], 0, 0, ["L16"])
+    iota(T.COLK[:], [[0, 24], [1, 8]], 0, 0, ["COLK"])
+    iota(T.KC1[0:32, :], [[-1024, 4], [0, 8], [-128, 8]], 33 * 128, 0, ["KC1"])
+    iota(T.KT[:], [[-1, 64]], 33, 0, ["KT"])
+    iota(T.COLG[:], [[1, 8], [0, 16]], 0, 0, ["COLG"])
+    iota(T.COLL[:], [[0, 8], [1, 16]], 0, 0, ["COLL"])
+    send(nxt, "p", 0, T.SP[:], T.S0[:], ["S0", "LO3", "HI3"], "r_p")
+    ms(T.ONE[0:32, :], 1.0, ["ONE"])
+    ms(T.KC2[0:32, :], float(2 ** 28), ["KC2"])
+    ms(T.CB[:], BIG, ["CB"])
+    ms(T.A[:, W:TW], C, ["Ax"])
+    ms(T.LO[:, W:TW], 0.0, ["LOx"])
+    ms(T.EF[:, SPARE:TW], 0.0, ["EFd"])
+    ts(T.PI[:, 1:2], T.PI[:, 0:1], 15, None, Op.bitwise_and, None, ["PI0"], ["PI1"])
+    ts(T.PI[:, 2:3], T.PI[:, 0:1], 4, None, Op.arith_shift_right, None, ["PI0"], ["PI2"])
+    cp(T.PC[:, 0:3], T.PI[:, 0:3], ["PI0", "PI1", "PI2"], ["PC"])
+    pp, pl, pg = T.PC[:, 0:1], T.PC[:, 1:2], T.PC[:, 2:3]
+    ts(T.MG[:], T.COL[:, 0:8], pg, None, Op.is_equal, None, ["COL", "PC"], ["MG"])
+    ts(T.PC[:, 3:4], pg, 16.0, 15.0, Op.mult, Op.add, ["PC"], ["PC3"])
+    ts(T.ID[:], T.COL[:, 0:128], pp, None, Op.is_equal, None, ["COL", "PC"], ["ID"])
+    ts(T.NI[:], T.COL[:, 0:128], pp, -1.0, Op.is_equal, Op.mult, ["COL", "PC"], ["NI"])
+    ts(T.NS[:], T.COL[:, 0:128], pp, -1.0 / 1024, Op.is_equal, Op.mult, ["COL", "PC"], ["NS"])
+    ts(T.BIGM[:], T.COL[:], T.PC[:, 3:4], -BIG, Op.is_equal, Op.mult, ["COL", "PC3"], ["BIGM"])
+    ts(T.NM[:], T.COL[:, 0:16], pl, -1.0, Op.is_equal, Op.mult, ["COL", "PC"], ["NM"])
+    weights = [
+        lambda: cp(T.WF[:], T.WT[:], ["WT"], ["WF"]),
+        lambda: ts(T.WI[:], T.K2[:], T.WF[:, 1:2], T.WF[:, 0:1], Op.mult, Op.add, ["K2", "WF"], ["WI"]),
+        lambda: ts(T.WJ[:], T.WI[:], W - 1, None, Op.bitwise_and, None, ["WI"], ["WJ"]),
+        lambda: cp(T.WG[:], T.WJ[:], ["WJ"], ["WG"]),
+        lambda: cp(T.WH[:], T.WG[:], ["WG"], ["WH"]),
+    ]
+
+    def late_constants():
+        ts(T.ZK[:, 199:256:8], T.L16[:], pl, float(4096 + OWN), Op.add, Op.add, ["L16", "PC"], ["ZKs"])
+        ts(T.LNP[:], T.L16[:], pl, 1024.0, Op.add, Op.add, ["L16", "PC"], ["LNP"])
+        ts(T.DUM[:], T.L16[:], pl, float(SPARE), Op.add, Op.add, ["L16", "PC"], ["DUM"])
+        ts(T.RK[:], T.COLK[:], 1.0, 1.0e9, Op.min, Op.mult, ["COLK"], ["RK"])
+
+    def later_constants():
+        ts(T.IS[:], T.COL[:, 0:128], pp, 1.0 / 1024, Op.is_equal, Op.mult, ["COL", "PC"], ["IS"])
+        ts(T.NBLK[:], T.COLG[:], pg, -1.0, Op.is_equal, Op.mult, ["COLG", "PC"], ["NBLK"])
+        ts(T.CM[:], T.COLL[:], pl, None, Op.is_equal, None, ["COLL", "PC"], ["CM"])
+        ts(T.RST[:], T.COLL[:], 1.0, 2.0, Op.min, Op.mult, ["COLL"], ["RST"])
+
+    At = ["A0", "A1", "A2", "A3", "A4"]
+    LOt = ["LO0", "LO1", "LO2", "LO3"]
+    EFr = ["EF", "EFx", "EFd"]
+    SMr = ["SM%d" % k for k in range(8)]
+    near = prv in topo.cores_of(core)
+    put_off = []
+
+    def pack(k):
+        nm, bk, c0, c1 = [("pP", T.pP[:], 0, 512), ("pC", T.pC[:], 512, 1024), ("pA", T.pA[:], 1024, 1536),
+                          ("pN", T.pN[:, 0:2], 1536, 1792), ("pK", T.pK[:, 0:2], 1792, 2048)][k]
+        mm(bk, T.NI[:], T.LO[:, c0:c1], True, False, ["NI", LOt[c0 // 512]], [nm])
+        mm(bk, T.NS[:], T.HI[:, c0:c1], False, True, ["NS", "HI%d" % (c0 // 512)], [nm])
+        if k >= 2:
+            ts(T.A[:, c0:c1], bk, C, None, Op.add, None, [nm], [At[k]])
+        else:
+            act(T.A[:, c0:c1], bk, Act.Identity, [nm], [At[k]], bias=C)
+
+    for t in range(ST):
+        s_, St = "S%d" % t, T["S%d" % t]
+
+        def repeat(h):
+            nm, bk = ("pN", T.pN) if h == 0 else ("pK", T.pK)
+            for j in range(8):
+                mm(bk[:, :, j, :], T.ID[:], St[:, 64 * h:64 * h + 64], True, True, ["ID", s_], [nm])
+            act(T.B[:, 512 * h:512 * h + 512], bk[:], Act.Identity, [nm], ["B%d" % h], scale=1025.0 / 1024)
+
+        def stride():
+            tt(T.VD[:], T.XI[:, 1:64:8], T.XI[:, 0:64:8], Op.subtract, ["XI"], ["VD"])
+
+        for k in range(8):
+            if k < (8 if near and t > 0 else 5):
+                if t == 0:
+                    weights[k]()
+                ts(T.SM[:, :, k, :], St[:], T.MG[:, k:k + 1], None, Op.mult, None, [s_, "MG"], [SMr[k]])
+            else:
+                act(T.SM[:, :, k, :], St[:], Act.Identity, [s_, "MG"], [SMr[k]], scale=T.MG[:, k:k + 1])
+        repeat(0)
+        if t == 0:
+            repeat(1)
+            pack(0)
+        for a in range(8):
+            mm(T.pX[:, 0:4, a, :], T.SM[:, a], T.WH[:], True, True, SMr + ["WH"], ["pX"])
+        if t == 0:
+            late_constants()
+        else:
+            repeat(1)
+        if 1 <= t <= 3:
+            k = t - 1
+            tt(T.DD[:], T.DUM[:], T.PL[:, 8 * k:8 * k + 8], Op.subtract, ["DUM", "PL%d" % k], ["DD"])
+            tt(T.D[:, 8 * k:8 * k + 8], T.DD[:], T.FA[:, 8 * k:8 * k + 8], Op.mult, ["DD", "FA%d" % k], ["D%d" % k])
+        tt(T.X0[:], T.pX[:, 0:4], T.KTAB[:], Op.add, ["pX", "KTAB"], ["X0"])
+        ts(T.XI[:], T.X0[:], W - 1, None, Op.bitwise_and, None, ["X0"], ["XI"])
+        if t == 1:
+            cp(T.XU[:, 0:64], T.XI[:, 0:64], ["XI"], ["XU0"])
+            cp(T.XU[:, 64:256], T.XI[:, 64:256], ["XI"], ["XU1"])
+        else:
+            cp(T.XU[:], T.XI[:], ["XI"], ["XU0", "XU1"])
+        if t == 0:
+            for k in range(1, 5):
+                pack(k)
+        mm(T.pE[:, 0:3], T.ONE[0:32, :], T.KC1[0:32, 0:192], True, False, ["ONE", "KC1"], ["pE"])
+        mm(T.pE[:, 0:3], T.ONE[0:32, :], T.KC2[0:32, 0:192], False, False, ["ONE", "KC2"], ["pE"])
+        mm(T.pF[:, 0], T.ONE[0:32, :], T.KC1[0:32, 192:256], True, False, ["ONE", "KC1"], ["pF"])
+        mm(T.pF[:, 0], T.ONE[0:32, :], T.KC2[0:32, 192:256], False, False, ["ONE", "KC2"], ["pF"])
+        for a in range(8):
+            mm(T.pE[:, 0:3, a, :], T.SM[:, a], T.CB[:, 0:24], False, False, SMr + ["CB"], ["pE"])
+        for a in range(8):
+            mm(T.pF[:, 0, a, :], T.SM[:, a], T.CB[:, 0:8], False, False, SMr + ["CB"], ["pF"])
+        for f in put_off:
+            f()
+        put_off = []
+
+        def drift():
+            act(T.RR[:], St[:], Act.Relu, [s_, "D2"], ["RR"], bias=T.D2[:, t:t + 1], scale=-2.0)
+            act(T.EF[:, OWN:SPARE], T.RR[:], Act.Identity, ["RR", "ND"], ["EFx"], bias=T.ND[:, t:t + 1])
+
+        if t >= 2:
+            b_, Bt, k = "BL%d" % (t - 1), T["BL%d" % (t - 1)], t - 2
+            mm(T.pA[:, 0:128], T.NI[:], Bt[:, 0:128], True, False, ["NI", b_], ["pA"])
+            mm(T.pA[:, 0:128], T.IS[:], Bt[:, 128:256], False, True, ["IS", b_], ["pA"])
+            act(T.AC[:], T.pA[:, 0:128], Act.Identity, ["pA"], ["AC"], bias=C)
+            drift()
+            tt(T.O1[:], Bt[:, 256:264], T.D[:, 8 * k:8 * k + 8], Op.mult, [b_, "D%d" % k], ["O1"])
+            if t == 2:
+                stride()
+            tt(T.O2[:], T.DUM[:], T.O1[:], Op.subtract, ["DUM", "O1"], ["O2"])
+            cp(T.OU[:], T.O2[:], ["O2"], ["OU"])
+            cp(T.LO[:, 0:TW].indirect(T.OU[:, 0:8]), Bt[:, 0:128], [b_, "OU"], LOt + ["LOx"])
+            cp(T.A[:, 0:TW].indirect(T.OU[:, 0:8]), T.AC[:], ["AC", "OU"], At + ["Ax"])
+        for q in range(4):
+            cs, xu = slice(1024 * q, 1024 * q + 1024), "XU%d" % min(q, 1)
+            act(T.LG[:, cs], T.LO[:, 0:W].indirect(T.XU[:, 64 * q:64 * q + 64]), Act.Copy, LOt + [xu], ["LG%d" % q])
+            tt(T.PHI[:, cs], T.A[:, 0:W].indirect(T.XU[:, 64 * q:64 * q + 64]), T.B[:], Op.add, At + [xu, "B0", "B1"], ["PH%d" % q])
+            out, nm = (T.pE[:, q], "pE") if q < 3 else (T.pF[:, 0], "pF")
+            for buf, r in ((T.LG, "LG%d" % q), (T.PHI, "PH%d" % q)):
+                for j in range(16):
+                    last = q >= 2 and j == 15 and buf is T.PHI
+                    mm(out, T.BIGM[:, 15 - j:143 - j], buf[:, 1024 * q + j:1024 * q + 1024:16], False, last, [r, "BIGM"], [nm])
+        if t == 0:
+            act(T.D2[:, 0:ST], T.DR[:, 0:ST], Act.Identity, ["DR"], ["D2"], scale=2.0)
+            act(T.ND[:, 0:ST], T.DR[:, 0:ST], Act.Identity, ["DR"], ["ND"], scale=-1.0)
+        if t <= 1:
+            drift()
+        if 1 <= t <= 3:
+            mm(T.pC[:, 0:128], T.ID[:], T.CM[:], True, False, ["ID", "CM"], ["pC"])
+        tt(T.KEY[:, 0:192], T.pE[:, 0:3], T.XI[:, 0:192], Op.add, ["pE", "XI"], ["KEY0"])
+        if t >= 2:
+            cp(T.EF[:, 0:TW].indirect(T.OU[:, 0:8]), T["BE%d" % (t - 1)][:], ["BE%d" % (t - 1), "OU"], EFr)
+        else:
+            stride()
+        scan(T.ZK[:, 0:192], T.RK[:], T.KEY[:, 0:192], ["RK", "KEY0"], ["ZK"])
+
+        def three():
+            tt(T.R2[:], T.ZK[:, 7:128:8], T.ZK[:, 135:256:8], Op.max, ["ZK", "ZKs"], ["R2"])
+
+        def two():
+            tt(T.R1[:], T.R2[:, 0:8], T.R2[:, 8:16], Op.max, ["R2"], ["R1"])
+
+        if t <= 1:
+            three()
+        if t == 1:
+            two()
+        tt(T.KEY[:, 192:256], T.pF[:, 0], T.XI[:, 192:256], Op.add, ["pF", "XI"], ["KEY3"])
+        if t == 0:
+            two()
+        if t > 1:
+            three()
+        scan(T.ZL[:], T.RK[:, 0:64], T.KEY[:, 192:256], ["RK", "KEY3"], ["ZL"])
+        if t > 1:
+            two()
+        tt(T.KI[:], T.ZL[:, 7:64:8], T.R1[:], Op.max, ["ZL", "R1"], ["KI"])
+        KR = T.KR[:]
+        if t < ST - 1:
+            tt(KR, T.ZL[:, 7:64:8], T.R1[:], Op.max, ["ZL", "R1"], ["KR"])
+        ts(T.CK[:, 0:8], T.KI[:], 4095, None, Op.bitwise_and, None, ["KI"], ["CI"])
+        ts(T.CK[:, 8:16], T.KI[:], 12, None, Op.arith_shift_right, None, ["KI"], ["KK"])
+        cp(T.CU[:], T.CK[:], ["CI", "KK"], ["CU"])
+        if t <= 2:
+            ts(T.FL[:], KR, 33 * 4096.0, None, Op.is_lt, None, ["KR"], ["FL"])
+        col = T.CU[:, 0:8]
+
+        def probe_numbers(t=t):
+            act(T.YP[:, 128 * t:128 * t + 128], T.KT[:, 0:64].indirect(T.CU[:, 8:16]), Act.Copy, ["KT", "CU"], ["YP%d" % t])
+
+        if t == ST - 1:
+            tt(T.YS[:], T.EF[:, 0:TW].indirect(col), St[:], Op.add, EFr + ["CU", s_], ["YS"])
+            dma("y", T.ys[:], T.YS[:], ["YS"], [], "d_ys")
+            probe_numbers()
+            dma("s", T.yp[:, 512:640], T.YP[0:128:16, 512:640], ["YP4"], [], "d_yp1")
+            break
+        so = "SO%d" % t
+        tt(T[so][:], T.EF[:, 0:TW].indirect(col), St[:], Op.add, EFr + ["CU", s_], [so])
+        send(nxt, "s", t, T["S%d" % (t + 1)][:], T[so][:], [so], "r_s%d" % (t + 1))
+        fb, Ft = "FB%d" % t, T["FB%d" % t]
+        k8 = slice(8 * t, 8 * t + 8)
+        if t >= 1:
+            cp(Ft[:, 0:128], T.LO[:, 0:TW].indirect(col), LOt + ["LOx", "CU"], [fb + "l"])
+        else:
+            act(Ft[:, 0:128], T.LO[:, 0:TW].indirect(col), Act.Copy, LOt + ["LOx", "CU"], [fb + "l"])
+        ts(T.G[:], T.A[:, 0:TW].indirect(col), C, 1024.0, Op.subtract, Op.mult, At + ["Ax", "CU"], ["G"])
+        if t <= 2:
+            tt(T.M1[:], T.FL[:], T.VD[:], Op.mult, ["FL", "VD"], ["M1"])
+        if t >= 1:
+            al, aq, Al, ms_, Mt = "AL%d" % (t - 1), "AQ%d" % (t - 1), T["AL%d" % (t - 1)], "MS%d" % t, T["MS%d" % t]
+            act(T.FS[:], KR, Act.Relu, ["KR"], ["FS"], bias=-8191.0)
+            for a in range(8):
+                act(T.SC[:, EO[a]:EO[a] + EW[a]], Al[:, 384 + EO[a]:384 + EO[a] + EW[a]], Act.Identity, [aq, "FS"], ["SC%d" % a],
+                    scale=T.FS[:, a:a + 1])
+
+            def ef_a(out, nm, plus, minus):
+                if t == 1:
+                    mm(out, plus[:], St[:], True, False, ["ID", "NI", s_], [nm])
+                    mm(out, minus[:], T.SP[:], False, False, ["ID", "NI", "SP"], [nm])
+                else:
+                    mm(out, plus[:], Al[:, 256:384], True, False, ["ID", "NI", al], [nm])
+
+            ef_a(T.pP[:, 0:128], "pP", T.NI, T.ID)
+            ef_a(T.pA[:, 0:128], "pA", T.ID, T.NI)
+            for a in range(5):
+                mm(T.pC[:, 16 * a:128], T.NBLK[:], T.SC[:, EO[a]:EO[a] + EW[a]], False, False, ["NBLK", "SC%d" % a], ["pC"])
+            mm(T.pP[:, 0:128], T.ID[:], Ft[:, 0:128], False, True, ["ID", fb + "l"], ["pP"])
+            ef_a(T.pP[:, 128:256], "pP", T.ID, T.NI)
+            mm(T.pP[:, 128:256], T.IK[:], Ft[:, 0:128], False, False, ["IK", fb + "l"], ["pP"])
+            for a in range(5, 8):
+                mm(T.pC[:, 16 * a:128], T.NBLK[:], T.SC[:, EO[a]:EO[a] + EW[a]], False, a == 7, ["NBLK", "SC%d" % a], ["pC"])
+            mm(T.pP[:, 128:256], T.I4[:], T.G[:], False, True, ["I4", "G"], ["pP"])
+            mm(T.pA[:, 0:128], T.NI[:], St[:], False, False, ["NI", s_], ["pA"])
+            mm(T.pA[:, 0:128], T.ID[:], T[so][:], False, True, ["ID", so], ["pA"])
+            scan(T.Z[:], T.RST[:], T.pC[:, 0:128], ["RST", "pC"], ["Z"])
+            if t <= 2:
+                tt(T.P1[:], T.CK[:, 0:8], T.M1[:], Op.subtract, ["CI", "M1"], ["P1"])
+            tt(Mt[:, 256:264], T.Z[:, 15:128:16], T.FS[:], Op.min, ["Z", "FS"], [ms_ + "w"])
+            tt(Mt[:, 0:256], T.pP[:, 0:256], Al[:, 0:256], Op.max, ["pP", al], [ms_])
+            send(prv, "b", t, T["BL%d" % t][:], Mt[:], [ms_, ms_ + "w"], "r_b%d" % t)
+            act(T["ME%d" % t][:], T.pA[:, 0:128], Act.Copy, ["pA"], ["ME%d" % t])
+            send(prv, "e", t, T["BE%d" % t][:], T["ME%d" % t][:], ["ME%d" % t], "r_e%d" % t)
+        if t <= 2:
+            if t == 0:
+                ts(T.IK[:], T.COL[:, 0:128], pp, 1024.0, Op.is_equal, Op.mult, ["COL", "PC"], ["IK"])
+                tt(T.P1[:], T.CK[:, 0:8], T.M1[:], Op.subtract, ["CI", "M1"], ["P1"])
+                ts(T.I4[:], T.COL[:, 0:128], pp, None, Op.is_equal, None, ["COL", "PC"], ["I4"])
+            ts(T.PL[:, k8], T.P1[:], W - 1, None, Op.bitwise_and, None, ["P1"], ["PL%d" % t])
+            if t == 0:
+                ts(T.BLK[:], T.COLG[:], pg, None, Op.is_equal, None, ["COLG", "PC"], ["BLK"])
+            ts(T.FA[:, k8], KR, 8192.0, None, Op.is_ge, None, ["KR"], ["FA%d" % t])
+            ts(T.T1[:], T.PL[:, k8], -256.0, None, Op.mult, None, ["PL%d" % t], ["T1"])
+            tt(T.NK[:], T.T1[:], T.LNP[:], Op.subtract, ["T1", "LNP"], ["NK"])
+            if t >= 1:
+                act(Ft[:, 256:384], T.EF[:, 0:TW].indirect(col), Act.Copy, EFr + ["CU"], [fb + "e"])
+            mm(T.pN[:, 0], T.IK[:], Ft[:, 0:128], True, False, ["IK", fb + "l"], ["pN"])
+            mm(T.pN[:, 0], T.I4[:], T.G[:], False, True, ["I4", "G"], ["pN"])
+            act(Ft[:, 128:256], T.pN[:, 0], Act.Copy, ["pN"], [fb + "h"])
+            wd = 384 if t >= 1 else 256
+            send(nxt, "a", t, T["AL%d" % t][:, 0:wd], Ft[:, 0:wd], [fb + x for x in "lhe"], "r_a%d" % t)
+            for a in range(8):
+                o = T.PD[:, 16 * a:16 * a + 16]
+                if a < 5:
+                    ts(o, T.NM[:], T.NK[:, a:a + 1], -4.0, Op.mult, Op.add, ["NM", "NK"], ["PD%d" % a])
+                else:
+                    act(o, T.NM[:], Act.Identity, ["NM", "NK"], ["PD%d" % a], bias=-4.0, scale=T.NK[:, a:a + 1])
+            mm(T.pK[:, 0], T.BLK[:], T.PD[:], True, True, ["BLK"] + ["PD%d" % a for a in range(8)], ["pK"])
+            if t == 0:
+                later_constants()
+            for a in range(8):
+                act(T.TA[:, EO[a]:EO[a] + EW[a]], T.pK[:, 0, a:8, :], Act.Abs, ["pK", "NK", "FA%d" % t], ["TA%d" % a],
+                    bias=T.NK[:, a:a + 1], scale=T.FA[:, 8 * t + a:8 * t + a + 1])
+
+            def shared(t=t, Ft=Ft, fb=fb):
+                act(Ft[:, 384:384 + EN], T.TA[:], Act.Relu, ["TA%d" % a for a in range(8)], [fb + "q"], bias=64.0, scale=-1.0)
+                send(nxt, "q", t, T["AL%d" % t][:, 384:384 + EN], Ft[:, 384:384 + EN], [fb + "q"], "r_q%d" % t)
+
+            if t == 0:
+                shared()
+                probe_numbers()
+            else:
+                put_off = [shared, probe_numbers]
+        else:
+            probe_numbers()
+            dma("y", T.yp[:, 0:512], T.YP[0:128:16, 0:512], ["YP%d" % k for k in range(4)], [], "d_yp0")
+
+    wait("g", list(total.items()))

@@ -1,52 +1,57 @@
+from concourse.bass import DstId, RemoteDMATransfer
 from concourse.mybir import AluOpType as Op, ActivationFunctionType as Act
 
 W, L, ST = 2048, 128, 5
-OWN, SPARE, TW = 2048, 2176, 2304
-C = 1024.5 - 1.0 / 2048
-BIG = float(2 ** 19)
+SPARE, OWN, TW = 2048, 2176, 2304
+EPS = 1.0 / 1024
+CH = 768.25 - EPS / 2
+HS = 448
+BIG = float(2 ** 23)
+MAGIC = 1.5 * 2 ** 23
+BLOCK = 2 ** 18
+NG, NS_ = 8, 3
+ORDER = ("states w_open fill masks_s masks_v kept probes again_a fill fill fill ask whole_a rest_a fill e e offsets_a again_b "
+         "e e fill whole_b rest_b e e lows e e fill w_bounds u_lows w_lows offsets_b lowest repeat0 u w served addend scatter "
+         "repeat1")
+LOADS = [(0, 1024), (1024, 1792), (1792, 2048)]
+PACKS = [(0, 512), (512, 1024), (1024, 1408), (1408, 1792), (1792, 1920), (1920, 2048)]
 EW = [128 - 16 * a for a in range(8)]
 EO = [sum(EW[:a]) for a in range(8)]
-EN = sum(EW)
 F32, BF, F16, I32, U16 = "float32", "bfloat16", "float16", "int32", "uint16"
 SCRATCH = {}
 for _d, _names in (
-        (F32, dict(A=TW, WF=2, D2=8, ND=8, WG=32, PC=4, COL=144, COLG=128, COLL=128, COLK=192, K2=32, KTAB=256, KT=64, L16=8,
-                   LNP=8, DUM=8, MG=8, NM=16, RST=128, RK=192, I4=128, BLK=128, B=1024, KEY=256, ZK=256, ZL=64, R2=16, R1=8, KR=8,
-                   G=128, FS=8, Z=128, VD=8, FL=8, M1=8, FA=24, T1=8, NK=8, DD=8, D=24, PD=128, TA=EN, O1=8, O2=8, AC=128,
-                   YS=128, YP=640)),
-        (BF, dict(LO=TW, EF=TW, HI=W, DR=8, KC1=256, KC2=256, ONE=128, CB=32, CM=128, ID=128, NI=128, IK=128, IS=128, NS=128,
-                  NBLK=128, BIGM=144, RR=128, LG=4096, SC=EN, FB3=128, SP=128)),
-        (F16, dict(WH=32, PHI=4096)),
-        (I32, dict(WT=2, WI=32, WJ=32, PI=4, X0=256, XI=256, KI=8, CK=16, P1=8, PL=24)),
-        (U16, dict(XU=256, CU=16, OU=8))):
+        (F32, dict(A=TW, NUM=TW, WF=2, D2=8, ND=8, WG=32, PC=5, COL=144, COLL=128, K2=32, KA=256, KB=256, L16=8, THR=8,
+                   MG=8, RSD=128, I4=128, N4=128, T1=128, B=1024, Z=264, R2=16, R1=8, KN=8, FL=8, VD=8,
+                   M1=8, PLT=24, AP=8, ZD=128, U=128, UW=128, YS=128, YP=640)),
+        (BF, dict(LO=W, HI=W, EF=TW, DR=8, KE=192, ONE=128, CM=128, ID=128, NI=128, IS=128, NS=128, BLK=128,
+                  TRI=128, BP=144, BN=144, RR=128, E=sum(EW), MS=384)),
+        (F16, dict(WH=32, WN=32, KP=256, KQ=256, RD=256, PHI=4096, H=4096, NA=384, NB=128, PB=384)),
+        (I32, dict(WT=2, WI=32, WJ=32, PI=4, CI=16, P1=8, PL=8, CK=16)),
+        (U16, dict(CU=16, PU=16, OU=8))):
     for _k, _n in _names.items():
         SCRATCH[_k] = ("sbuf", [128, _n], _d)
-SCRATCH["SM"] = ("sbuf", [128, 8, 8, 16], BF)
-for _k, _s in dict(pX=[8, 8, 8], pE=[8, 8, 8], pF=[8, 8, 8], pN=[4, 8, 16], pK=[4, 8, 16], pP=[512], pC=[512], pA=[512]).items():
+SCRATCH["SM"] = ("sbuf", [128, 8, NG, 16], BF)
+for _k, _s in dict(pX=[8, 8, 8], pN=[4, 8, 16], pK=[4, 8, 16], pE=[512], pF=[512], pD=[512], pU=[512], pY=[8, 8, 8]).items():
     SCRATCH[_k] = ("psum", [128] + _s, F32)
-for _k, _ts, _n in (("S", range(5), 128),
-                    ("SO", range(4), 128),
-                    ("FB", range(3), 384 + EN),
-                    ("AL", range(3), 384 + EN),
-                    ("MS", range(1, 4), 264),
-                    ("BL", range(1, 4), 264),
-                    ("ME", range(1, 4), 128),
-                    ("BE", range(1, 4), 128)):
+for _k, _ts, _n, _d in (("S", range(5), 128, BF),
+                        ("SO", range(4), 128, BF),
+                        ("XA", range(5), 64, U16),
+                        ("XB", range(5), 192, U16),
+                        ("KEY", range(5), 256, F32),
+                        ("KI", range(5), 8, I32),
+                        ("G", range(4), 128, F32),
+                        ("KN", range(1, 4), 8, I32),
+                        ("GN", range(1, 4), 128, F32),
+                        ("SN", range(1, 4), 128, BF)):
     for _t in _ts:
-        SCRATCH["%s%d" % (_k, _t)] = ("sbuf", [128, _n], BF)
+        SCRATCH["%s%d" % (_k, _t)] = ("sbuf", [128, _n], _d)
 
-SEMAPHORES = (["qg", "qv", "qs", "qp", "sent", "d_s0", "d_wt", "d_dr", "d_ef", "d_ys", "d_yp0", "d_yp1", "r_p"]
-              + ["d_lo%d" % k for k in range(4)] + ["d_hi%d" % k for k in range(4)]
-              + ["r_s%d" % t for t in range(1, 5)] + ["r_a%d" % t for t in range(3)] + ["r_q%d" % t for t in range(3)]
-              + ["r_b%d" % t for t in range(1, 4)] + ["r_e%d" % t for t in range(1, 4)])
-
-
-def _engines(topo, cores, r, kind, t):
-    n = len(cores)
-    fwd, back = topo.mask(cores[r % n], cores[(r + 1) % n]), topo.mask(cores[r % n], cores[(r - 1) % n])
-    if kind in "psaq":
-        return fwd
-    return fwd & back if (kind, t) == ("b", 1) else back
+for _k in ("XA", "XB", "KEY"):
+    SCRATCH["O" + _k] = ("sbuf", [128, 4, SCRATCH[_k + "0"][1][1]], SCRATCH[_k + "0"][2])
+SEMAPHORES = (["qg", "qv", "qs", "qp", "sent", "d_s0", "d_wt", "d_dr", "d_ef", "d_ys", "d_yp0", "d_yp1"]
+              + ["d_%s%d" % (x, k) for x in ("lo", "hi") for k in range(len(LOADS))]
+              + ["r_WN"] + ["r_%s%d" % (k, t) for k in ("S", "XA", "XB", "KEY") for t in range(1, 5)]
+              + ["r_%s%d" % (k, t) for k in ("KN", "GN", "SN") for t in range(1, 4)])
 
 
 def rank_program(g, core, T, topo):
@@ -95,16 +100,37 @@ def rank_program(g, core, T, topo):
     def dma(q, out, in_, r, w, sem):
         op(q, lambda: Q[q].dma_start(out, in_), r, w, sem, 16)
 
-    def send(dst, kind, t, out, in_, r, sem):
-        mask = _engines(topo, T.cores, rank, kind, t)
+    def near(c):
+        return c in topo.cores_of(core)
+
+    def engines(src, dst):
+        far = [c for c in T.cores if c not in topo.cores_of(src)][0]
+        return topo.mask(src, dst) & ~topo.mask(src, far) or topo.mask(src, dst)
+
+    def send(dst, name, in_, r):
+        mask = engines(core, dst)
         wait("g", [k for x in r for k in wrote.get(x, [])])
         rid, pid = topo.addr(dst, core)
-        g.remote_dma(out, in_, T.sem[sem], T.sem["sent"], pid, rid, mask)
+        g.remote_dma(T[name][:], in_, T.sem["r_" + name], T.sem["sent"], pid, rid, mask)
         total["sent"] = total.get("sent", 0) + bin(mask).count("1")
 
-    def lands(x, sem, r, kind, t):
-        k = bin(_engines(topo, T.cores, r, kind, t)).count("1")
-        wrote[x], total[sem] = [(sem, k)], k
+    def send_together(msgs):
+        transfers = []
+        for dst, name, in_, r, pieces in msgs:
+            wait("g", [k for x in r for k in wrote.get(x, [])])
+            rid, pid = topo.addr(dst, core)
+            es = [e for e in topo.engines(core, dst) if engines(core, dst) >> e & 1]
+            wd, ne = in_.shape[1] // pieces, len(es) // pieces
+            for i in range(pieces):
+                transfers.append(RemoteDMATransfer(
+                    dst_ids=[DstId(rid=rid, pnc=pid)], dma_engine_mask=sum(1 << e for e in es[ne * i:ne * i + ne]),
+                    remote_sem=T.sem["r_" + name], src=in_[:, wd * i:wd * i + wd], dst=T[name][:, wd * i:wd * i + wd]))
+            total["sent"] = total.get("sent", 0) + len(es)
+        g.remote_dma_fused(transfers, local_sem=T.sem["sent"])
+
+    def lands(name, src):
+        k = bin(engines(src, core)).count("1")
+        wrote[name], total["r_" + name] = [("r_" + name, k)], k
 
     V, S, P = g.vector, g.scalar, g.tensor
 
@@ -123,8 +149,8 @@ def rank_program(g, core, T, topo):
     def ms(out, c, w):
         op("v", lambda: V.memset(out, c), [], w)
 
-    def scan(out, d0, d1, r, w):
-        op("v", lambda: V.tensor_tensor_scan(out, d0, d1, 0.0, Op.min, Op.max), r, w)
+    def scan(out, d0, d1, first, o0, o1, r, w):
+        op("v", lambda: V.tensor_tensor_scan(out, d0, d1, first, o0, o1), r, w)
 
     def act(out, a, f, r, w, bias=0.0, scale=1.0):
         op("s", lambda: S.activation(out, a, f, bias=bias, scale=scale), r, w)
@@ -138,310 +164,359 @@ def rank_program(g, core, T, topo):
         else:
             op("g", lambda: g.iota(out, pat, base, cm, allow_small_or_imprecise_dtypes=True), [], w)
 
-    lands("SP", "r_p", rank - 1, "p", 0)
-    for t in range(4):
-        lands("S%d" % (t + 1), "r_s%d" % (t + 1), rank - 1, "s", t)
-    for t in range(3):
-        lands("AL%d" % t, "r_a%d" % t, rank - 1, "a", t)
-        lands("AQ%d" % t, "r_q%d" % t, rank - 1, "q", t)
-        lands("BL%d" % (t + 1), "r_b%d" % (t + 1), rank + 1, "b", t + 1)
-        lands("BE%d" % (t + 1), "r_e%d" % (t + 1), rank + 1, "e", t + 1)
+    lands("WN", nxt)
+    for t in range(1, 5):
+        for k in ("S", "XA", "XB", "KEY"):
+            lands("%s%d" % (k, t), prv)
+    for t in range(1, 4):
+        for k in ("KN", "GN", "SN"):
+            lands("%s%d" % (k, t), nxt)
 
     dma("y", T.S0[:], T.s0[:], [], ["S0"], "d_s0")
     dma("s", T.WT[:], T.wt[:], [], ["WT"], "d_wt")
-    for h in range(4):
-        cs = slice(512 * h, 512 * h + 512)
+    for h, (c0, c1) in enumerate(LOADS):
+        cs = slice(c0, c1)
         dma("y", T.LO[:, cs], T.lo[:, cs], [], ["LO%d" % h], "d_lo%d" % h)
         dma("s", T.HI[:, cs], T.hi[:, cs], [], ["HI%d" % h], "d_hi%d" % h)
-    dma("y", T.DR[:, 0:ST], T.dr[:], ["HI3"], ["DR"], "d_dr")
-    dma("y", T.EF[:, 0:W], T.ef[:], ["HI3"], ["EF"], "d_ef")
+    last = "HI%d" % (len(LOADS) - 1)
+    dma("y", T.DR[:, 0:ST], T.dr[:], [last], ["DR"], "d_dr")
+    dma("y", T.EF[:, 0:W], T.ef[:], [last], ["EF"], "d_ef")
 
     iota(T.PI[:, 0:1], [[0, 1]], 0, 1, ["PI0"], True)
     iota(T.COL[:], [[1, 144]], 0, 0, ["COL"])
-    iota(T.K2[:], [[2, 32]], 0, 0, ["K2"])
-    iota(T.KTAB[:], [[8, 4], [0, 8], [1, 8]], 0, 0, ["KTAB"])
+    iota(T.K2[:], [[-2, 32]], 62, 0, ["K2"])
+    iota(T.KA[0:32, :], [[-16, 4], [0, 8], [-2, 8]], 63 - W, 0, ["KA"])
+    iota(T.KB[0:32, :], [[-16, 4], [-BLOCK // W, 8], [-2, 8]], 62 + 7 * BLOCK // W, 0, ["KB"])
     iota(T.L16[:], [[16, 8]], 0, 0, ["L16"])
-    iota(T.COLK[:], [[0, 24], [1, 8]], 0, 0, ["COLK"])
-    iota(T.KC1[0:32, :], [[-1024, 4], [0, 8], [-128, 8]], 33 * 128, 0, ["KC1"])
-    iota(T.KT[:], [[-1, 64]], 33, 0, ["KT"])
-    iota(T.COLG[:], [[1, 8], [0, 16]], 0, 0, ["COLG"])
     iota(T.COLL[:], [[0, 8], [1, 16]], 0, 0, ["COLL"])
-    send(nxt, "p", 0, T.SP[:], T.S0[:], ["S0", "LO3", "HI3"], "r_p")
+    iota(T.NUM[:, 0:W], [[1, W]], 0, 0, ["NUM"])
     ms(T.ONE[0:32, :], 1.0, ["ONE"])
-    ms(T.KC2[0:32, :], float(2 ** 28), ["KC2"])
-    ms(T.CB[:], BIG, ["CB"])
-    ms(T.A[:, W:TW], C, ["Ax"])
-    ms(T.LO[:, W:TW], 0.0, ["LOx"])
-    ms(T.EF[:, SPARE:TW], 0.0, ["EFd"])
+    ms(T.KE[0:32, :], -BIG * 128, ["KE"])
+    ms(T.A[:, W:TW], 0.0, ["Ax"])
+    ms(T.EF[:, SPARE:OWN], 0.0, ["EFd"])
     ts(T.PI[:, 1:2], T.PI[:, 0:1], 15, None, Op.bitwise_and, None, ["PI0"], ["PI1"])
     ts(T.PI[:, 2:3], T.PI[:, 0:1], 4, None, Op.arith_shift_right, None, ["PI0"], ["PI2"])
-    cp(T.PC[:, 0:3], T.PI[:, 0:3], ["PI0", "PI1", "PI2"], ["PC"])
+    ts(T.PI[:, 3:4], T.PI[:, 0:1], 4, NG - 1, Op.arith_shift_right, Op.bitwise_and, ["PI0"], ["PI3"])
+    ms(T.RSD[:], 0.0, ["RSD"])
+    ms(T.BLK[:], 4096.0, ["BLK"])
+    cp(T.PC[:, 0:4], T.PI[:, 0:4], ["PI0", "PI1", "PI2", "PI3"], ["PC"])
+    ms(T.NUM[:, W:TW], 4094.0, ["NUMx"])
     pp, pl, pg = T.PC[:, 0:1], T.PC[:, 1:2], T.PC[:, 2:3]
-    ts(T.MG[:], T.COL[:, 0:8], pg, None, Op.is_equal, None, ["COL", "PC"], ["MG"])
-    ts(T.PC[:, 3:4], pg, 16.0, 15.0, Op.mult, Op.add, ["PC"], ["PC3"])
-    ts(T.ID[:], T.COL[:, 0:128], pp, None, Op.is_equal, None, ["COL", "PC"], ["ID"])
-    ts(T.NI[:], T.COL[:, 0:128], pp, -1.0, Op.is_equal, Op.mult, ["COL", "PC"], ["NI"])
-    ts(T.NS[:], T.COL[:, 0:128], pp, -1.0 / 1024, Op.is_equal, Op.mult, ["COL", "PC"], ["NS"])
-    ts(T.BIGM[:], T.COL[:], T.PC[:, 3:4], -BIG, Op.is_equal, Op.mult, ["COL", "PC3"], ["BIGM"])
-    ts(T.NM[:], T.COL[:, 0:16], pl, -1.0, Op.is_equal, Op.mult, ["COL", "PC"], ["NM"])
+
+    def diagonal(name, c):
+        ts(T[name][:], T.COL[:, 0:128], pp, c, Op.is_equal, Op.mult, ["COL", "PC"], [name])
+
+    ts(T.MG[:], T.COL[:, 0:8], T.PC[:, 3:4], None, Op.is_equal, None, ["COL", "PC"], ["MG"])
+    ts(T.PC[:, 4:5], pg, 16.0, 15.0, Op.mult, Op.add, ["PC"], ["PC3"])
+    diagonal("ID", 1.0)
+    diagonal("NI", -1.0)
+    diagonal("NS", -EPS)
+    ts(T.KP[0:32, :], T.KA[0:32, :], 1.0 / (4096 * 32), None, Op.mult, None, ["KA"], ["KP"])
     weights = [
         lambda: cp(T.WF[:], T.WT[:], ["WT"], ["WF"]),
-        lambda: ts(T.WI[:], T.K2[:], T.WF[:, 1:2], T.WF[:, 0:1], Op.mult, Op.add, ["K2", "WF"], ["WI"]),
+        lambda: ts(T.WG[:], T.K2[:], T.WF[:, 1:2], T.WF[:, 0:1], Op.mult, Op.add, ["K2", "WF"], ["WG"]),
+        lambda: ts(T.WI[:], T.WG[:], W / 2, None, Op.add, None, ["WG"], ["WI"]),
         lambda: ts(T.WJ[:], T.WI[:], W - 1, None, Op.bitwise_and, None, ["WI"], ["WJ"]),
-        lambda: cp(T.WG[:], T.WJ[:], ["WJ"], ["WG"]),
-        lambda: cp(T.WH[:], T.WG[:], ["WG"], ["WH"]),
+        lambda: ts(T.WH[:], T.WJ[:], -W / 2, 1.0 / W, Op.add, Op.mult, ["WJ"], ["WH"]),
     ]
 
-    def late_constants():
-        ts(T.ZK[:, 199:256:8], T.L16[:], pl, float(4096 + OWN), Op.add, Op.add, ["L16", "PC"], ["ZKs"])
-        ts(T.LNP[:], T.L16[:], pl, 1024.0, Op.add, Op.add, ["L16", "PC"], ["LNP"])
-        ts(T.DUM[:], T.L16[:], pl, float(SPARE), Op.add, Op.add, ["L16", "PC"], ["DUM"])
-        ts(T.RK[:], T.COLK[:], 1.0, 1.0e9, Op.min, Op.mult, ["COLK"], ["RK"])
+    def test_constants():
+        ts(T.BP[:], T.COL[:], T.PC[:, 4:5], BIG, Op.is_equal, Op.mult, ["COL", "PC3"], ["BP"])
+        ts(T.BN[:], T.COL[:], T.PC[:, 4:5], -BIG, Op.is_equal, Op.mult, ["COL", "PC3"], ["BN"])
+        ts(T.KQ[0:32, :], T.KB[0:32, :], 1.0 / 32, None, Op.mult, None, ["KB"], ["KQ"])
+        ts(T.THR[:], T.L16[:], -BLOCK / 16, 7.0 * BLOCK + 32 * 4096, Op.mult, Op.add, ["L16"], ["THR"])
+        ts(T.R1[:], T.L16[:], pl, float(OWN), Op.add, Op.add, ["L16", "PC"], ["R1"])
+        ts(T.RSD[:, 0:128:16], T.L16[:], pl, float(SPARE), Op.add, Op.add, ["L16", "PC", "RSD"], ["RSD"])
+        tt(T.Z[:, 199:256:8], T.R1[:], T.THR[:], Op.add, ["R1", "THR"], ["Zn"])
 
-    def later_constants():
-        ts(T.IS[:], T.COL[:, 0:128], pp, 1.0 / 1024, Op.is_equal, Op.mult, ["COL", "PC"], ["IS"])
-        ts(T.NBLK[:], T.COLG[:], pg, -1.0, Op.is_equal, Op.mult, ["COLG", "PC"], ["NBLK"])
-        ts(T.CM[:], T.COLL[:], pl, None, Op.is_equal, None, ["COLL", "PC"], ["CM"])
-        ts(T.RST[:], T.COLL[:], 1.0, 2.0, Op.min, Op.mult, ["COLL"], ["RST"])
+    def select(out, in_, pat, how, other, base, cm):
+        op("g", lambda: g.affine_select(T[out][:], T[in_][:], pat, how, other, base, cm), [in_], [out])
 
-    At = ["A0", "A1", "A2", "A3", "A4"]
-    LOt = ["LO0", "LO1", "LO2", "LO3"]
+    def compose_constants():
+        for name, c in (("IS", EPS), ("I4", 1.0), ("N4", -1.0)):
+            act(T[name][:], T.ID[:], Act.Identity, ["ID"], [name], scale=c)
+        act(T.T1[:], T.COLL[:], Act.Abs, ["COLL", "PC"], ["T1"], bias=pl, scale=-1.0)
+        act(T.CM[:], T.T1[:], Act.Identity, ["T1"], ["CM"], bias=4096.0, scale=61440.0)
+        select("BLK", "BLK", [[16, 8], [0, 16]], Op.is_ge, 0.0, 15, -1)
+        select("BLK", "BLK", [[-16, 8], [0, 16]], Op.is_ge, 0.0, 0, 1)
+        select("TRI", "BLK", [[1, 128]], Op.is_gt, 0.0, 0, -1)
+        select("TRI", "TRI", [[1, 128]], Op.not_equal, -4096.0, 0, -1)
+
+    At = ["A%d" % k for k in range(len(PACKS))] + ["Ax"]
     EFr = ["EF", "EFx", "EFd"]
-    SMr = ["SM%d" % k for k in range(8)]
-    near = prv in topo.cores_of(core)
-    put_off = []
+    SMr = ["SM%d" % k for k in range(NG)]
 
     def pack(k):
-        nm, bk, c0, c1 = [("pP", T.pP[:], 0, 512), ("pC", T.pC[:], 512, 1024), ("pA", T.pA[:], 1024, 1536),
-                          ("pN", T.pN[:, 0:2], 1536, 1792), ("pK", T.pK[:, 0:2], 1792, 2048)][k]
-        mm(bk, T.NI[:], T.LO[:, c0:c1], True, False, ["NI", LOt[c0 // 512]], [nm])
-        mm(bk, T.NS[:], T.HI[:, c0:c1], False, True, ["NS", "HI%d" % (c0 // 512)], [nm])
-        if k >= 2:
-            ts(T.A[:, c0:c1], bk, C, None, Op.add, None, [nm], [At[k]])
+        nm, (c0, c1) = ["pD", "pU", "pE", "pF"][k % 4], PACKS[k]
+        h = [i for i in range(len(LOADS)) if LOADS[i][0] <= c0][-1]
+        out = T[nm][:, 0:c1 - c0]
+        mm(out, T.NI[:], T.LO[:, c0:c1], True, False, ["NI", "LO%d" % h], [nm])
+        mm(out, T.NS[:], T.HI[:, c0:c1], False, True, ["NS", "HI%d" % h], [nm])
+        if k % 2:
+            cp(T.A[:, c0:c1], out, [nm], [At[k]])
         else:
-            act(T.A[:, c0:c1], bk, Act.Identity, [nm], [At[k]], bias=C)
+            act(T.A[:, c0:c1], out, Act.Copy, [nm], [At[k]])
 
-    for t in range(ST):
-        s_, St = "S%d" % t, T["S%d" % t]
-
-        def repeat(h):
-            nm, bk = ("pN", T.pN) if h == 0 else ("pK", T.pK)
-            for j in range(8):
-                mm(bk[:, :, j, :], T.ID[:], St[:, 64 * h:64 * h + 64], True, True, ["ID", s_], [nm])
-            act(T.B[:, 512 * h:512 * h + 512], bk[:], Act.Identity, [nm], ["B%d" % h], scale=1025.0 / 1024)
-
-        def stride():
-            tt(T.VD[:], T.XI[:, 1:64:8], T.XI[:, 0:64:8], Op.subtract, ["XI"], ["VD"])
-
-        for k in range(8):
-            if k < (8 if near and t > 0 else 5):
-                if t == 0:
-                    weights[k]()
-                ts(T.SM[:, :, k, :], St[:], T.MG[:, k:k + 1], None, Op.mult, None, [s_, "MG"], [SMr[k]])
+    def blocks(s, ks, q):
+        for k in ks:
+            if q == "v":
+                ts(T.SM[:, :, k, :], T[s][:], T.MG[:, k:k + 1], None, Op.mult, None, [s, "MG"], [SMr[k]])
             else:
-                act(T.SM[:, :, k, :], St[:], Act.Identity, [s_, "MG"], [SMr[k]], scale=T.MG[:, k:k + 1])
-        repeat(0)
-        if t == 0:
-            repeat(1)
-            pack(0)
+                act(T.SM[:, :, k, :], T[s][:], Act.Identity, [s, "MG"], [SMr[k]], scale=T.MG[:, k:k + 1])
+
+    def repeat(t, h):
+        nm = ["pN", "pK"][h]
+        for j in range(8):
+            mm(T[nm][:, :, j, :], T.ID[:], T["S%d" % t][:, 64 * h:64 * h + 64], True, True, ["ID", "S%d" % t], [nm])
+
+    def addend(h):
+        nm = ["pN", "pK"][h]
+        act(T.B[:, 512 * h:512 * h + 512], T[nm][:], Act.Identity, [nm], ["B%d" % h], bias=CH, scale=1 + EPS)
+
+    EIGHTS = dict(pX=(0, 4), pF=(0, 1), pY=(1, 4))
+
+    def part(nm, a=None):
+        q0, q1 = EIGHTS[nm]
+        if nm == "pF":
+            return T.pF[:, 0:64] if a is None else T.pF[:, 8 * a:8 * a + 8]
+        return T[nm][:, q0:q1] if a is None else T[nm][:, q0:q1, a, :]
+
+    def begin(nm, more=()):
+        q0, q1 = EIGHTS[nm]
+        for i, c in enumerate(("KP",) + more):
+            mm(part(nm), T.ONE[0:32, :], T[c][0:32, 64 * q0:64 * q1], i == 0, False, ["ONE", c], [nm])
+
+    def linear(nm, w, stop):
+        q0, q1 = EIGHTS[nm]
         for a in range(8):
-            mm(T.pX[:, 0:4, a, :], T.SM[:, a], T.WH[:], True, True, SMr + ["WH"], ["pX"])
-        if t == 0:
-            late_constants()
-        else:
-            repeat(1)
+            mm(part(nm, a), T.SM[:, a], T[w][:, 8 * q0:8 * q1], False, stop and a == 7, SMr + [w], [nm])
+
+    def whole_part(nm):
+        q0, q1 = EIGHTS[nm]
+        ts(T.RD[:, 64 * q0:64 * q1], T.pX[:, q0:q1], MAGIC, MAGIC, Op.add, Op.subtract, ["pX"], ["RD" + nm])
+
+    def remainder(nm):
+        q0, q1 = EIGHTS[nm]
+        mm(part(nm), T.NI[:], T.RD[:, 64 * q0:64 * q1], False, True, ["NI"] + (["RDpF", "RDpY"] if nm == "pX" else ["RD" + nm]), [nm])
+
+    def hand_on(name, t):
+        return (name + "0", T[name + "0"][:]) if t == 0 else ("O%s%d" % (name, t), T["O" + name][:, t - 1])
+
+    def offsets(nm, t):
+        name = dict(pF="XA", pY="XB")[nm]
+        out, ap = hand_on(name, t)
+        ts(ap, part(nm), float(W), W / 2 - 0.5, Op.mult, Op.add, [nm], [out])
+        if t > 0:
+            send(nxt, "%s%d" % (name, t), ap, [out])
+
+    def keys(t):
+        begin("pX", ("KQ",))
+        linear("pX", "WN" if t else "WH", False)
+        remainder("pX")
+        out, ap = hand_on("KEY", t)
+        act(ap, T.pX[:, 0:4], Act.Identity, ["pX"], [out], bias=W / 2 - 0.5, scale=float(W))
+        if t > 0:
+            send(nxt, "KEY%d" % t, ap, [out])
+
+    def sums(out, nm, wt, buf, c0, r, stop=False):
+        for j in range(16):
+            mm(out, T[wt][:, 15 - j:143 - j], buf[:, c0 + j:c0 + 1024:16], False, stop and j == 15, r + [wt], [nm])
+
+    def tests(t):
+        def probe(c0, c1, add, r, w):
+            x, o = ("XA%d" % t, 0) if c0 < 1024 else ("XB%d" % t, 64)
+            tt(T.PHI[:, c0:c1], T.A[:, 0:W].indirect(T[x][:, c0 // 16 - o:c1 // 16 - o]), add, Op.add, At + [x] + r, [w])
+
+        def halves(q):
+            act(T.H[:, 1024 * q:1024 * q + 1024], T.PHI[:, 1024 * q:1024 * q + 1024], Act.Identity, PH[q], ["H%d" % q], bias=256.3)
+            sums(T.pE[:, 64 * q:64 * q + 64], "pE", "BP", T.H, 1024 * q, ["H%d" % q], q == 2)
+
+        PH = [["PHa", "PH0"], ["PH1"], ["PH2"], ["PH3"]]
+        probe(0, 512, T.B[:, 0:512], ["B0"], "PHa")
+        if t > 0:
+            addend(1)
+        probe(512, 1024, T.B[:, 512:1024], ["B1"], "PH0")
+        for q in range(1, 4):
+            probe(1024 * q, 1024 * q + 1024, T.B[:], ["B0", "B1"], "PH%d" % q)
+        keys(t)
         if 1 <= t <= 3:
-            k = t - 1
-            tt(T.DD[:], T.DUM[:], T.PL[:, 8 * k:8 * k + 8], Op.subtract, ["DUM", "PL%d" % k], ["DD"])
-            tt(T.D[:, 8 * k:8 * k + 8], T.DD[:], T.FA[:, 8 * k:8 * k + 8], Op.mult, ["DD", "FA%d" % k], ["D%d" % k])
-        tt(T.X0[:], T.pX[:, 0:4], T.KTAB[:], Op.add, ["pX", "KTAB"], ["X0"])
-        ts(T.XI[:], T.X0[:], W - 1, None, Op.bitwise_and, None, ["X0"], ["XI"])
-        if t == 1:
-            cp(T.XU[:, 0:64], T.XI[:, 0:64], ["XI"], ["XU0"])
-            cp(T.XU[:, 64:256], T.XI[:, 64:256], ["XI"], ["XU1"])
-        else:
-            cp(T.XU[:], T.XI[:], ["XI"], ["XU0", "XU1"])
-        if t == 0:
-            for k in range(1, 5):
-                pack(k)
-        mm(T.pE[:, 0:3], T.ONE[0:32, :], T.KC1[0:32, 0:192], True, False, ["ONE", "KC1"], ["pE"])
-        mm(T.pE[:, 0:3], T.ONE[0:32, :], T.KC2[0:32, 0:192], False, False, ["ONE", "KC2"], ["pE"])
-        mm(T.pF[:, 0], T.ONE[0:32, :], T.KC1[0:32, 192:256], True, False, ["ONE", "KC1"], ["pF"])
-        mm(T.pF[:, 0], T.ONE[0:32, :], T.KC2[0:32, 192:256], False, False, ["ONE", "KC2"], ["pF"])
-        for a in range(8):
-            mm(T.pE[:, 0:3, a, :], T.SM[:, a], T.CB[:, 0:24], False, False, SMr + ["CB"], ["pE"])
-        for a in range(8):
-            mm(T.pF[:, 0, a, :], T.SM[:, a], T.CB[:, 0:8], False, False, SMr + ["CB"], ["pF"])
-        for f in put_off:
-            f()
-        put_off = []
-
-        def drift():
-            act(T.RR[:], St[:], Act.Relu, [s_, "D2"], ["RR"], bias=T.D2[:, t:t + 1], scale=-2.0)
-            act(T.EF[:, OWN:SPARE], T.RR[:], Act.Identity, ["RR", "ND"], ["EFx"], bias=T.ND[:, t:t + 1])
-
-        if t >= 2:
-            b_, Bt, k = "BL%d" % (t - 1), T["BL%d" % (t - 1)], t - 2
-            mm(T.pA[:, 0:128], T.NI[:], Bt[:, 0:128], True, False, ["NI", b_], ["pA"])
-            mm(T.pA[:, 0:128], T.IS[:], Bt[:, 128:256], False, True, ["IS", b_], ["pA"])
-            act(T.AC[:], T.pA[:, 0:128], Act.Identity, ["pA"], ["AC"], bias=C)
-            drift()
-            tt(T.O1[:], Bt[:, 256:264], T.D[:, 8 * k:8 * k + 8], Op.mult, [b_, "D%d" % k], ["O1"])
-            if t == 2:
-                stride()
-            tt(T.O2[:], T.DUM[:], T.O1[:], Op.subtract, ["DUM", "O1"], ["O2"])
-            cp(T.OU[:], T.O2[:], ["O2"], ["OU"])
-            cp(T.LO[:, 0:TW].indirect(T.OU[:, 0:8]), Bt[:, 0:128], [b_, "OU"], LOt + ["LOx"])
-            cp(T.A[:, 0:TW].indirect(T.OU[:, 0:8]), T.AC[:], ["AC", "OU"], At + ["Ax"])
-        for q in range(4):
-            cs, xu = slice(1024 * q, 1024 * q + 1024), "XU%d" % min(q, 1)
-            act(T.LG[:, cs], T.LO[:, 0:W].indirect(T.XU[:, 64 * q:64 * q + 64]), Act.Copy, LOt + [xu], ["LG%d" % q])
-            tt(T.PHI[:, cs], T.A[:, 0:W].indirect(T.XU[:, 64 * q:64 * q + 64]), T.B[:], Op.add, At + [xu, "B0", "B1"], ["PH%d" % q])
-            out, nm = (T.pE[:, q], "pE") if q < 3 else (T.pF[:, 0], "pF")
-            for buf, r in ((T.LG, "LG%d" % q), (T.PHI, "PH%d" % q)):
-                for j in range(16):
-                    last = q >= 2 and j == 15 and buf is T.PHI
-                    mm(out, T.BIGM[:, 15 - j:143 - j], buf[:, 1024 * q + j:1024 * q + 1024:16], False, last, [r, "BIGM"], [nm])
+            places(t - 1)
+        if t >= 1:
+            numbers(t - 1, T.PU[:, 8:16])
+        mm(T.pE[:, 0:192], T.ONE[0:32, :], T.KE[0:32, :], True, False, ["ONE", "KE"], ["pE"])
+        mm(T.pF[:, 0:64], T.ONE[0:32, :], T.KE[0:32, 0:64], True, False, ["ONE", "KE"], ["pF"])
         if t == 0:
             act(T.D2[:, 0:ST], T.DR[:, 0:ST], Act.Identity, ["DR"], ["D2"], scale=2.0)
             act(T.ND[:, 0:ST], T.DR[:, 0:ST], Act.Identity, ["DR"], ["ND"], scale=-1.0)
-        if t <= 1:
-            drift()
-        if 1 <= t <= 3:
-            mm(T.pC[:, 0:128], T.ID[:], T.CM[:], True, False, ["ID", "CM"], ["pC"])
-        tt(T.KEY[:, 0:192], T.pE[:, 0:3], T.XI[:, 0:192], Op.add, ["pE", "XI"], ["KEY0"])
+            compose_constants()
+        for q in range(3):
+            sums(T.pE[:, 64 * q:64 * q + 64], "pE", "BN", T.PHI, 1024 * q, PH[q])
+            halves(q)
+            if q == 1:
+                drift(t)
+        sums(T.pF[:, 0:64], "pF", "BN", T.PHI, 3072, ["PH3"])
+        act(T.H[:, 3072:3072 + HS], T.PHI[:, 3072:3072 + HS], Act.Identity, ["PH3"], ["H3s"], bias=256.3)
+        ts(T.H[:, 3072 + HS:4096], T.PHI[:, 3072 + HS:4096], 256.3, None, Op.add, None, ["PH3"], ["H3v"])
+        sums(T.pF[:, 0:64], "pF", "BP", T.H, 3072, ["H3s", "H3v"], True)
+
+    def first_hit(t):
         if t >= 2:
-            cp(T.EF[:, 0:TW].indirect(T.OU[:, 0:8]), T["BE%d" % (t - 1)][:], ["BE%d" % (t - 1), "OU"], EFr)
-        else:
-            stride()
-        scan(T.ZK[:, 0:192], T.RK[:], T.KEY[:, 0:192], ["RK", "KEY0"], ["ZK"])
+            tt(T.EF[:, 0:TW].indirect(T.OU[:, 0:8]), T["SN%d" % (t - 1)][:], T.MS[:, 128 * (t - 2):128 * (t - 1)], Op.add,
+               ["SN%d" % (t - 1), "MS%d" % (t - 2), "OU"], EFr)
+        for q in range(3):
+            cs = slice(64 * q, 64 * q + 64)
+            scan(T.Z[:, cs], T.pE[:, cs], T["KEY%d" % t][:, cs], BIG, Op.min, Op.max, ["pE", "KEY%d" % t], ["Z%d" % q])
+        tt(T.R2[:], T.Z[:, 7:128:8], T.Z[:, 135:256:8], Op.min, ["Z0", "Z1", "Z2", "Zn"], ["R2"])
+        tt(T.R1[:], T.R2[:, 0:8], T.R2[:, 8:16], Op.min, ["R2"], ["R1"])
+        scan(T.ZD[:, 0:64], T.pF[:, 0:64], T["KEY%d" % t][:, 192:256], BIG, Op.min, Op.max, ["pF", "KEY%d" % t], ["ZD"])
+        tt(T["KI%d" % t][:], T.ZD[:, 7:64:8], T.R1[:], Op.min, ["ZD", "R1"], ["KI%d" % t])
 
-        def three():
-            tt(T.R2[:], T.ZK[:, 7:128:8], T.ZK[:, 135:256:8], Op.max, ["ZK", "ZKs"], ["R2"])
+    def drift(t):
+        act(T.RR[:], T["S%d" % t][:], Act.Relu, ["S%d" % t, "D2"], ["RR"], bias=T.D2[:, t:t + 1], scale=-2.0)
+        act(T.EF[:, OWN:TW], T.RR[:], Act.Identity, ["RR", "ND"], ["EFx"], bias=T.ND[:, t:t + 1])
 
-        def two():
-            tt(T.R1[:], T.R2[:, 0:8], T.R2[:, 8:16], Op.max, ["R2"], ["R1"])
+    def numbers(t, o):
+        act(T.YP[:, 128 * t:128 * t + 128], T.COL[:, 0:64].indirect(o), Act.Copy, ["COL", "PU", "CU"], ["YP%d" % t])
 
-        if t <= 1:
-            three()
-        if t == 1:
-            two()
-        tt(T.KEY[:, 192:256], T.pF[:, 0], T.XI[:, 192:256], Op.add, ["pF", "XI"], ["KEY3"])
-        if t == 0:
-            two()
-        if t > 1:
-            three()
-        scan(T.ZL[:], T.RK[:, 0:64], T.KEY[:, 192:256], ["RK", "KEY3"], ["ZL"])
-        if t > 1:
-            two()
-        tt(T.KI[:], T.ZL[:, 7:64:8], T.R1[:], Op.max, ["ZL", "R1"], ["KI"])
-        KR = T.KR[:]
-        if t < ST - 1:
-            tt(KR, T.ZL[:, 7:64:8], T.R1[:], Op.max, ["ZL", "R1"], ["KR"])
-        ts(T.CK[:, 0:8], T.KI[:], 4095, None, Op.bitwise_and, None, ["KI"], ["CI"])
-        ts(T.CK[:, 8:16], T.KI[:], 12, None, Op.arith_shift_right, None, ["KI"], ["KK"])
-        cp(T.CU[:], T.CK[:], ["CI", "KK"], ["CU"])
-        if t <= 2:
-            ts(T.FL[:], KR, 33 * 4096.0, None, Op.is_lt, None, ["KR"], ["FL"])
-        col = T.CU[:, 0:8]
+    def place(t):
+        ki, kn = T["KI%d" % t][:], "KI%d" % t
+        number = lambda: ts(T.CK[:, 8:16], ki, 12, 63, Op.arith_shift_right, Op.bitwise_and, [kn], ["KK"])
+        if t > 2:
+            return [number, lambda: cp(T.PU[:, 8:16], T.CK[:, 8:16], ["KK"], ["PU"])]
+        return [
+            lambda: tt(T.VD[:], T["KEY%d" % t][:, 198:256:8], T["KEY%d" % t][:, 199:256:8], Op.subtract, ["KEY%d" % t], ["VD"]),
+            number,
+            lambda: ts(T.FL[:], T.CK[:, 8:16], 1.0, None, Op.is_ge, None, ["KK"], ["FL"]),
+            lambda: tt(T.M1[:], T.FL[:], T.VD[:], Op.mult, ["FL", "VD"], ["M1"]),
+            lambda: tt(T.KN[:], ki, T.THR[:], Op.subtract, [kn, "THR"], ["KN"]),
+            lambda: tt(T.P1[:], ki, T.M1[:], Op.subtract, [kn, "M1"], ["P1"]),
+            lambda: ts(T.PL[:], T.P1[:], W - 1, None, Op.bitwise_and, None, ["P1"], ["PL"]),
+            lambda: tt(T.CK[:, 0:8], T.PL[:], T.KN[:], Op.max, ["PL", "KN"], ["PK"]),
+            lambda: cp(T.PU[:], T.CK[:], ["PK", "KK"], ["PU"]),
+            lambda: tt(T.PLT[:, 8 * t:8 * t + 8], T.CK[:, 0:8], T.THR[:], Op.add, ["PK", "THR"], ["PLT%d" % t])]
 
-        def probe_numbers(t=t):
-            act(T.YP[:, 128 * t:128 * t + 128], T.KT[:, 0:64].indirect(T.CU[:, 8:16]), Act.Copy, ["KT", "CU"], ["YP%d" % t])
+    def places(t):
+        act(T.PB[:, 128 * t:128 * t + 128], T.NUM[:, 0:TW].indirect(T.PU[:, 0:8]), Act.Copy, ["NUM", "NUMx", "PU"], ["PB%d" % t])
 
+    def kept(t):
+        cs = slice(128 * t, 128 * t + 128)
+        act(T.NA[:, cs], T["G%d" % t][:], Act.Identity, ["G%d" % t], ["NA%d" % t], bias=1280.0)
+        act(T.MS[:, cs], T["S%d" % t][:], Act.Identity, ["S%d" % t], ["MS%d" % t], scale=-1.0)
+
+    def open_sums(t):
+        k = t - 1
+        cs = slice(128 * k, 128 * k + 128)
+        mm(T.pD[:, 0:128], T.ID[:], T.PB[:, cs], True, False, ["ID", "PB%d" % k], ["pD"])
+        mm(T.pD[:, 0:128], T.ID[:], T.CM[:], False, False, ["ID", "CM"], ["pD"])
+        open_sum(t, "pU", T.pU[:, 0:128], ["I4", "NI", "ID", "NI"])
+
+    def open_sum(t, nm, out, ws):
+        k = t - 1
+        cs = slice(128 * k, 128 * k + 128)
+        for i, (x, r) in enumerate(((T["G%d" % k][:], "G%d" % k), (T.NA[:, cs], "NA%d" % k), (T["SO%d" % k][:], "SO%d" % k),
+                                    (T["S%d" % k][:], "S%d" % k))):
+            mm(out, T[ws[i]][:], x, i == 0, False, [ws[i], r], [nm])
+
+    def asked(t, a):
+        k = t - 1
+        ts(T.E[:, EO[a]:EO[a] + EW[a]], T.PB[:, 128 * k + 16 * a:128 * k + 128], float((7 - a) * BLOCK + 32 * 4096),
+           T.AP[:, a:a + 1], Op.add, Op.is_equal, ["PB%d" % k, "AP"], ["E%d" % a])
+        if a < 7:
+            mm(T.pD[:, 16 * a + 16:128], T.BLK[:], T.E[:, EO[a] + 16:EO[a] + EW[a]], False, False, ["BLK", "E%d" % a], ["pD"])
+        mm(T.pD[:, 16 * a:16 * a + 16], T.TRI[:], T.E[:, EO[a]:EO[a] + 16], False, a == 7, ["TRI", "E%d" % a], ["pD"])
+
+    blocks("S0", range(NG), "s")
+    for f in weights:
+        f()
+    send(prv, "WN", T.WH[:], ["WH"])
+    repeat(0, 0)
+    addend(0)
+    repeat(0, 1)
+    for nm in EIGHTS:
+        begin(nm)
+        linear(nm, "WH", nm == "pX")
+    addend(1)
+    for nm in ("pF", "pY"):
+        whole_part(nm)
+        remainder(nm)
+    test_constants()
+    for nm in ("pF", "pY"):
+        offsets(nm, 0)
+    for k in range(len(PACKS)):
+        pack(k)
+
+    for t in range(ST):
+        s_, St = "S%d" % t, T["S%d" % t]
+        tests(t)
         if t == ST - 1:
+            dma("y", T.yp[:, 0:512], T.YP[0:128:16, 0:512], ["YP%d" % k for k in range(4)], [], "d_yp0")
+        if 1 <= t <= 3:
+            open_sums(t)
+        first_hit(t)
+        if t < ST - 1:
+            for nm in ("pX", "pY", "pF"):
+                begin(nm)
+        later = place(t) if t < ST - 1 else []
+
+        def fill():
+            if later:
+                later.pop(0)()
+
+        ki, kn = T["KI%d" % t][:], "KI%d" % t
+        if 1 <= t <= 3:
+            send(prv, "KN%d" % t, ki, [kn])
+        fill()
+        ts(T.CI[:, 0:8], ki, 4095, None, Op.bitwise_and, None, [kn], ["CI"])
+        col = T.CU[:, 0:8]
+        if t == ST - 1:
+            ts(T.CI[:, 8:16], ki, 12, 63, Op.arith_shift_right, Op.bitwise_and, [kn], ["KK"])
+            cp(T.CU[:], T.CI[:], ["CI", "KK"], ["CU"])
             tt(T.YS[:], T.EF[:, 0:TW].indirect(col), St[:], Op.add, EFr + ["CU", s_], ["YS"])
             dma("y", T.ys[:], T.YS[:], ["YS"], [], "d_ys")
-            probe_numbers()
+            numbers(t, T.CU[:, 8:16])
             dma("s", T.yp[:, 512:640], T.YP[0:128:16, 512:640], ["YP4"], [], "d_yp1")
             break
-        so = "SO%d" % t
-        tt(T[so][:], T.EF[:, 0:TW].indirect(col), St[:], Op.add, EFr + ["CU", s_], [so])
-        send(nxt, "s", t, T["S%d" % (t + 1)][:], T[so][:], [so], "r_s%d" % (t + 1))
-        fb, Ft = "FB%d" % t, T["FB%d" % t]
-        k8 = slice(8 * t, 8 * t + 8)
-        if t >= 1:
-            cp(Ft[:, 0:128], T.LO[:, 0:TW].indirect(col), LOt + ["LOx", "CU"], [fb + "l"])
+        fill()
+        cp(col, T.CI[:, 0:8], ["CI"], ["CU"])
+        fill()
+        so, So, Gt = "SO%d" % t, T["SO%d" % t], T["G%d" % t][:]
+        tt(So[:], T.EF[:, 0:TW].indirect(col), St[:], Op.add, EFr + ["CU", s_], [so])
+        act(Gt, T.A[:, 0:TW].indirect(col), Act.Copy, At + ["CU"], ["G%d" % t])
+        if t == 0:
+            send(nxt, "S1", So[:], [so])
         else:
-            act(Ft[:, 0:128], T.LO[:, 0:TW].indirect(col), Act.Copy, LOt + ["LOx", "CU"], [fb + "l"])
-        ts(T.G[:], T.A[:, 0:TW].indirect(col), C, 1024.0, Op.subtract, Op.mult, At + ["Ax", "CU"], ["G"])
-        if t <= 2:
-            tt(T.M1[:], T.FL[:], T.VD[:], Op.mult, ["FL", "VD"], ["M1"])
-        if t >= 1:
-            al, aq, Al, ms_, Mt = "AL%d" % (t - 1), "AQ%d" % (t - 1), T["AL%d" % (t - 1)], "MS%d" % t, T["MS%d" % t]
-            act(T.FS[:], KR, Act.Relu, ["KR"], ["FS"], bias=-8191.0)
-            for a in range(8):
-                act(T.SC[:, EO[a]:EO[a] + EW[a]], Al[:, 384 + EO[a]:384 + EO[a] + EW[a]], Act.Identity, [aq, "FS"], ["SC%d" % a],
-                    scale=T.FS[:, a:a + 1])
-
-            def ef_a(out, nm, plus, minus):
-                if t == 1:
-                    mm(out, plus[:], St[:], True, False, ["ID", "NI", s_], [nm])
-                    mm(out, minus[:], T.SP[:], False, False, ["ID", "NI", "SP"], [nm])
-                else:
-                    mm(out, plus[:], Al[:, 256:384], True, False, ["ID", "NI", al], [nm])
-
-            ef_a(T.pP[:, 0:128], "pP", T.NI, T.ID)
-            ef_a(T.pA[:, 0:128], "pA", T.ID, T.NI)
-            for a in range(5):
-                mm(T.pC[:, 16 * a:128], T.NBLK[:], T.SC[:, EO[a]:EO[a] + EW[a]], False, False, ["NBLK", "SC%d" % a], ["pC"])
-            mm(T.pP[:, 0:128], T.ID[:], Ft[:, 0:128], False, True, ["ID", fb + "l"], ["pP"])
-            ef_a(T.pP[:, 128:256], "pP", T.ID, T.NI)
-            mm(T.pP[:, 128:256], T.IK[:], Ft[:, 0:128], False, False, ["IK", fb + "l"], ["pP"])
-            for a in range(5, 8):
-                mm(T.pC[:, 16 * a:128], T.NBLK[:], T.SC[:, EO[a]:EO[a] + EW[a]], False, a == 7, ["NBLK", "SC%d" % a], ["pC"])
-            mm(T.pP[:, 128:256], T.I4[:], T.G[:], False, True, ["I4", "G"], ["pP"])
-            mm(T.pA[:, 0:128], T.NI[:], St[:], False, False, ["NI", s_], ["pA"])
-            mm(T.pA[:, 0:128], T.ID[:], T[so][:], False, True, ["ID", so], ["pA"])
-            scan(T.Z[:], T.RST[:], T.pC[:, 0:128], ["RST", "pC"], ["Z"])
-            if t <= 2:
-                tt(T.P1[:], T.CK[:, 0:8], T.M1[:], Op.subtract, ["CI", "M1"], ["P1"])
-            tt(Mt[:, 256:264], T.Z[:, 15:128:16], T.FS[:], Op.min, ["Z", "FS"], [ms_ + "w"])
-            tt(Mt[:, 0:256], T.pP[:, 0:256], Al[:, 0:256], Op.max, ["pP", al], [ms_])
-            send(prv, "b", t, T["BL%d" % t][:], Mt[:], [ms_, ms_ + "w"], "r_b%d" % t)
-            act(T["ME%d" % t][:], T.pA[:, 0:128], Act.Copy, ["pA"], ["ME%d" % t])
-            send(prv, "e", t, T["BE%d" % t][:], T["ME%d" % t][:], ["ME%d" % t], "r_e%d" % t)
-        if t <= 2:
-            if t == 0:
-                ts(T.IK[:], T.COL[:, 0:128], pp, 1024.0, Op.is_equal, Op.mult, ["COL", "PC"], ["IK"])
-                tt(T.P1[:], T.CK[:, 0:8], T.M1[:], Op.subtract, ["CI", "M1"], ["P1"])
-                ts(T.I4[:], T.COL[:, 0:128], pp, None, Op.is_equal, None, ["COL", "PC"], ["I4"])
-            ts(T.PL[:, k8], T.P1[:], W - 1, None, Op.bitwise_and, None, ["P1"], ["PL%d" % t])
-            if t == 0:
-                ts(T.BLK[:], T.COLG[:], pg, None, Op.is_equal, None, ["COLG", "PC"], ["BLK"])
-            ts(T.FA[:, k8], KR, 8192.0, None, Op.is_ge, None, ["KR"], ["FA%d" % t])
-            ts(T.T1[:], T.PL[:, k8], -256.0, None, Op.mult, None, ["PL%d" % t], ["T1"])
-            tt(T.NK[:], T.T1[:], T.LNP[:], Op.subtract, ["T1", "LNP"], ["NK"])
-            if t >= 1:
-                act(Ft[:, 256:384], T.EF[:, 0:TW].indirect(col), Act.Copy, EFr + ["CU"], [fb + "e"])
-            mm(T.pN[:, 0], T.IK[:], Ft[:, 0:128], True, False, ["IK", fb + "l"], ["pN"])
-            mm(T.pN[:, 0], T.I4[:], T.G[:], False, True, ["I4", "G"], ["pN"])
-            act(Ft[:, 128:256], T.pN[:, 0], Act.Copy, ["pN"], [fb + "h"])
-            wd = 384 if t >= 1 else 256
-            send(nxt, "a", t, T["AL%d" % t][:, 0:wd], Ft[:, 0:wd], [fb + x for x in "lhe"], "r_a%d" % t)
-            for a in range(8):
-                o = T.PD[:, 16 * a:16 * a + 16]
-                if a < 5:
-                    ts(o, T.NM[:], T.NK[:, a:a + 1], -4.0, Op.mult, Op.add, ["NM", "NK"], ["PD%d" % a])
-                else:
-                    act(o, T.NM[:], Act.Identity, ["NM", "NK"], ["PD%d" % a], bias=-4.0, scale=T.NK[:, a:a + 1])
-            mm(T.pK[:, 0], T.BLK[:], T.PD[:], True, True, ["BLK"] + ["PD%d" % a for a in range(8)], ["pK"])
-            if t == 0:
-                later_constants()
-            for a in range(8):
-                act(T.TA[:, EO[a]:EO[a] + EW[a]], T.pK[:, 0, a:8, :], Act.Abs, ["pK", "NK", "FA%d" % t], ["TA%d" % a],
-                    bias=T.NK[:, a:a + 1], scale=T.FA[:, 8 * t + a:8 * t + a + 1])
-
-            def shared(t=t, Ft=Ft, fb=fb):
-                act(Ft[:, 384:384 + EN], T.TA[:], Act.Relu, ["TA%d" % a for a in range(8)], [fb + "q"], bias=64.0, scale=-1.0)
-                send(nxt, "q", t, T["AL%d" % t][:, 384:384 + EN], Ft[:, 384:384 + EN], [fb + "q"], "r_q%d" % t)
-
-            if t == 0:
-                shared()
-                probe_numbers()
-            else:
-                put_off = [shared, probe_numbers]
-        else:
-            probe_numbers()
-            dma("y", T.yp[:, 0:512], T.YP[0:128:16, 0:512], ["YP%d" % k for k in range(4)], [], "d_yp0")
+            send_together([(nxt, "S%d" % (t + 1), So, [so], 1), (prv, "GN%d" % t, T["G%d" % t], ["G%d" % t], 2)])
+        gn, ga = "GN%d" % t, "G%d" % (t - 1)
+        blocks_left = list(range(8))
+        forward = dict(
+            masks_s=lambda: blocks(so, range(0, NS_), "s"), masks_v=lambda: blocks(so, range(NS_, NG), "v"),
+            repeat0=lambda: repeat(t + 1, 0), repeat1=lambda: repeat(t + 1, 1), addend=lambda: addend(0),
+            probes=lambda: linear("pX", "WN", True),
+            again_a=lambda: linear("pF", "WN", False), again_b=lambda: linear("pY", "WN", False),
+            whole_a=lambda: whole_part("pF"), whole_b=lambda: whole_part("pY"),
+            rest_a=lambda: remainder("pF"), rest_b=lambda: remainder("pY"),
+            offsets_a=lambda: offsets("pF", t + 1), offsets_b=lambda: offsets("pY", t + 1),
+            fill=fill, kept=lambda: kept(t) if t <= 2 else None)
+        back = dict(
+            w_open=lambda: open_sum(t, "pE", T.pE[:, 256:384], ["N4", "ID", "IS", "NS"]),
+            states=lambda: send(prv, "SN%d" % t, So[:], [so]),
+            ask=lambda: tt(T.AP[:], T["KN%d" % t][:], T.PLT[:, 8 * t - 8:8 * t], Op.max, ["KN%d" % t, "PLT%d" % (t - 1)], ["AP"]),
+            e=lambda: asked(t, blocks_left.pop(0)),
+            lows=lambda: act(T.NB[:], T[gn][:], Act.Identity, [gn], ["NB"], bias=1280.0),
+            w_bounds=lambda: mm(T.pE[:, 256:384], T.I4[:], T[gn][:], False, False, ["I4", gn], ["pE"]),
+            u_lows=lambda: mm(T.pU[:, 0:128], T.ID[:], T.NB[:], False, True, ["ID", "NB"], ["pU"]),
+            w_lows=lambda: mm(T.pE[:, 256:384], T.NI[:], T.NB[:], False, True, ["NI", "NB"], ["pE"]),
+            u=lambda: tt(T.U[:], T.pU[:, 0:128], T[ga][:], Op.min, ["pU", ga], ["U"]),
+            w=lambda: act(T.UW[:], T.pE[:, 256:384], Act.Relu, ["pE"], ["UW"]),
+            lowest=lambda: scan(T.ZD[:], T.RSD[:], T.pD[:, 0:128], 0.0, Op.max, Op.min, ["RSD", "pD"], ["ZD"]),
+            served=lambda: cp(T.OU[:], T.ZD[:, 15:128:16], ["ZD"], ["OU"]),
+            scatter=lambda: tt(T.A[:, 0:TW].indirect(T.OU[:, 0:8]), T.U[:], T.UW[:], Op.add, ["U", "UW", "OU"], At))
+        for name in ORDER.split():
+            if name in forward:
+                forward[name]()
+            elif t >= 1:
+                back[name]()
+        while later:
+            fill()
 
     wait("g", list(total.items()))

@@ -5,32 +5,38 @@ W, L, ST = 2048, 128, 5
 SPARE, OWN, TW = 2048, 2176, 2304
 EPS = 1.0 / 1024
 CH = 768.25 - EPS / 2
-HS = 448
+HS = 256
 BIG = float(2 ** 23)
 MAGIC = 1.5 * 2 ** 23
 BLOCK = 2 ** 18
 NG, NS_ = 8, 3
-ORDER = ("states w_open fill masks_s masks_v kept probes again_a fill fill fill ask whole_a rest_a fill e e offsets_a again_b "
-         "e e fill whole_b rest_b e e lows e e fill w_bounds u_lows w_lows offsets_b lowest repeat0 u w served addend scatter "
-         "repeat1")
+EV = 3
+RAW = True
+ORDER = ("w_open fill masks_v masks_s apart probes fill again_a e e whole_a rest_a again_b fill e es es es es es whole_b lows "
+         "u_lows rest_b w_bounds w_lows w offsets_a repeat0 addend fill lowest offsets_b fill served u fill repeat1 scatter addend1 "
+         "kept |"
+         "w_open fill masks_v fill masks_s apart probes fill whole_a again_a rest_a again_b fill whole_b offsets_a es es rest_b e e "
+         "es es es e lows w_bounds u_lows w_lows offsets_b repeat0 lowest w fill repeat1 served addend addend1 u fill scatter kept")
+EFP = [(0, 2), (2, 6), (6, 8), (8, 8)]
 LOADS = [(0, 1024), (1024, 1792), (1792, 2048)]
 PACKS = [(0, 512), (512, 1024), (1024, 1408), (1408, 1792), (1792, 1920), (1920, 2048)]
-EW = [128 - 16 * a for a in range(8)]
-EO = [sum(EW[:a]) for a in range(8)]
 F32, BF, F16, I32, U16 = "float32", "bfloat16", "float16", "int32", "uint16"
 SCRATCH = {}
 for _d, _names in (
-        (F32, dict(A=TW, NUM=TW, WF=2, D2=8, ND=8, WG=32, PC=5, COL=144, COLL=128, K2=32, KA=256, KB=256, L16=8, THR=8,
-                   MG=8, RSD=128, I4=128, N4=128, T1=128, B=1024, Z=264, R2=16, R1=8, KN=8, FL=8, VD=8,
-                   M1=8, PLT=24, AP=8, ZD=128, U=128, UW=128, YS=128, YP=640)),
+        (F32, dict(A=TW, NUM=TW, WF=2, D2=16, WG=32, PC=5, COL=144, COLL=128, K2=32, KA=256, KB=256, L16=8, THR=8,
+                   MG=8, RSD=128, I4=128, N4=128, PF=24, B=1024, Z=264, R2=16, R1=8, FL=8, VD=8,
+                   M1=8, RW=512, ZD=128, U=128, UW=128, YS=128, YP=640)),
         (BF, dict(LO=W, HI=W, EF=TW, DR=8, KE=192, ONE=128, CM=128, ID=128, NI=128, IS=128, NS=128, BLK=128,
-                  TRI=128, BP=144, BN=144, RR=128, E=sum(EW), MS=384)),
-        (F16, dict(WH=32, WN=32, KP=256, KQ=256, RD=256, PHI=4096, H=4096, NA=384, NB=128, PB=384)),
-        (I32, dict(WT=2, WI=32, WJ=32, PI=4, CI=16, P1=8, PL=8, CK=16)),
+                  TRI=128, BP=144, BN=144, RR=128, MS=384)),
+        (F16, dict(WH=32, WN=32, IE=128, KP=256, KQ=256, RD=256, PHI=4096, H=4096, NA=384, NB=128, PB=384)),
+        (I32, dict(WT=2, WI=32, WJ=32, PI=4, CI=16, P1=8, PL=8, CK=16, KM=8, KI=8)),
         (U16, dict(CU=16, PU=16, OU=8))):
     for _k, _n in _names.items():
         SCRATCH[_k] = ("sbuf", [128, _n], _d)
-SCRATCH["SM"] = ("sbuf", [128, 8, NG, 16], BF)
+SCRATCH["SM"] = ("sbuf", [128, 8, 8, 16], BF)
+SCRATCH["FA"] = ("sbuf", [128, 3, 8], F32)
+SCRATCH["E"] = ("sbuf", [128, 8, 128], BF)
+SCRATCH["EA"] = ("sbuf", [128, 8, 128], F32)
 for _k, _s in dict(pX=[8, 8, 8], pN=[4, 8, 16], pK=[4, 8, 16], pE=[512], pF=[512], pD=[512], pU=[512], pY=[8, 8, 8]).items():
     SCRATCH[_k] = ("psum", [128] + _s, F32)
 for _k, _ts, _n, _d in (("S", range(5), 128, BF),
@@ -38,9 +44,8 @@ for _k, _ts, _n, _d in (("S", range(5), 128, BF),
                         ("XA", range(5), 64, U16),
                         ("XB", range(5), 192, U16),
                         ("KEY", range(5), 256, F32),
-                        ("KI", range(5), 8, I32),
                         ("G", range(4), 128, F32),
-                        ("KN", range(1, 4), 8, I32),
+                        ("FN", range(1, 4), 8, F32),
                         ("GN", range(1, 4), 128, F32),
                         ("SN", range(1, 4), 128, BF)):
     for _t in _ts:
@@ -51,7 +56,7 @@ for _k in ("XA", "XB", "KEY"):
 SEMAPHORES = (["qg", "qv", "qs", "qp", "sent", "d_s0", "d_wt", "d_dr", "d_ef", "d_ys", "d_yp0", "d_yp1"]
               + ["d_%s%d" % (x, k) for x in ("lo", "hi") for k in range(len(LOADS))]
               + ["r_WN"] + ["r_%s%d" % (k, t) for k in ("S", "XA", "XB", "KEY") for t in range(1, 5)]
-              + ["r_%s%d" % (k, t) for k in ("KN", "GN", "SN") for t in range(1, 4)])
+              + ["r_%s%d" % (k, t) for k in ("FN", "GN", "SN") for t in range(1, 4)])
 
 
 def rank_program(g, core, T, topo):
@@ -103,12 +108,14 @@ def rank_program(g, core, T, topo):
     def near(c):
         return c in topo.cores_of(core)
 
-    def engines(src, dst):
-        far = [c for c in T.cores if c not in topo.cores_of(src)][0]
-        return topo.mask(src, dst) & ~topo.mask(src, far) or topo.mask(src, dst)
+    def engines(src, dst, name=""):
+        far = topo.mask(src, [c for c in T.cores if c not in topo.cores_of(src)][0])
+        if name == "WN":
+            return topo.mask(src, dst)
+        return far if name in ("S1", "XA1", "XB1") else topo.mask(src, dst) & ~far or far
 
     def send(dst, name, in_, r):
-        mask = engines(core, dst)
+        mask = engines(core, dst, name)
         wait("g", [k for x in r for k in wrote.get(x, [])])
         rid, pid = topo.addr(dst, core)
         g.remote_dma(T[name][:], in_, T.sem["r_" + name], T.sem["sent"], pid, rid, mask)
@@ -129,7 +136,7 @@ def rank_program(g, core, T, topo):
         g.remote_dma_fused(transfers, local_sem=T.sem["sent"])
 
     def lands(name, src):
-        k = bin(engines(src, core)).count("1")
+        k = bin(engines(src, core, name)).count("1")
         wrote[name], total["r_" + name] = [("r_" + name, k)], k
 
     V, S, P = g.vector, g.scalar, g.tensor
@@ -169,7 +176,7 @@ def rank_program(g, core, T, topo):
         for k in ("S", "XA", "XB", "KEY"):
             lands("%s%d" % (k, t), prv)
     for t in range(1, 4):
-        for k in ("KN", "GN", "SN"):
+        for k in ("FN", "GN", "SN"):
             lands("%s%d" % (k, t), nxt)
 
     dma("y", T.S0[:], T.s0[:], [], ["S0"], "d_s0")
@@ -192,26 +199,26 @@ def rank_program(g, core, T, topo):
     iota(T.NUM[:, 0:W], [[1, W]], 0, 0, ["NUM"])
     ms(T.ONE[0:32, :], 1.0, ["ONE"])
     ms(T.KE[0:32, :], -BIG * 128, ["KE"])
-    ms(T.A[:, W:TW], 0.0, ["Ax"])
-    ms(T.EF[:, SPARE:OWN], 0.0, ["EFd"])
     ts(T.PI[:, 1:2], T.PI[:, 0:1], 15, None, Op.bitwise_and, None, ["PI0"], ["PI1"])
     ts(T.PI[:, 2:3], T.PI[:, 0:1], 4, None, Op.arith_shift_right, None, ["PI0"], ["PI2"])
-    ts(T.PI[:, 3:4], T.PI[:, 0:1], 4, NG - 1, Op.arith_shift_right, Op.bitwise_and, ["PI0"], ["PI3"])
     ms(T.RSD[:], 0.0, ["RSD"])
+    cp(T.PC[:, 0:3], T.PI[:, 0:3], ["PI0", "PI1", "PI2"], ["PC"])
     ms(T.BLK[:], 4096.0, ["BLK"])
-    cp(T.PC[:, 0:4], T.PI[:, 0:4], ["PI0", "PI1", "PI2", "PI3"], ["PC"])
-    ms(T.NUM[:, W:TW], 4094.0, ["NUMx"])
+    ms(T.EF[:, SPARE:OWN], 0.0, ["EFd"])
     pp, pl, pg = T.PC[:, 0:1], T.PC[:, 1:2], T.PC[:, 2:3]
+    ts(T.ID[:], T.COL[:, 0:128], pp, None, Op.is_equal, None, ["COL", "PC"], ["ID"])
+    ts(T.MG[:], T.COL[:, 0:8], pg, None, Op.is_equal, None, ["COL", "PC"], ["MG"])
+    ts(T.PC[:, 3:4], pg, 16.0, 15.0, Op.mult, Op.add, ["PC"], ["PC3"])
+    ms(T.A[:, W:TW], 0.0, ["Ax"])
+    ts(T.BP[:], T.COL[:], T.PC[:, 3:4], BIG, Op.is_equal, Op.mult, ["COL", "PC3"], ["BP"])
 
-    def diagonal(name, c):
-        ts(T[name][:], T.COL[:, 0:128], pp, c, Op.is_equal, Op.mult, ["COL", "PC"], [name])
+    def scaled(out, in_, c, ps=slice(0, 128)):
+        act(T[out][ps, :], T[in_][ps, :], Act.Identity, [in_], [out], scale=c)
 
-    ts(T.MG[:], T.COL[:, 0:8], T.PC[:, 3:4], None, Op.is_equal, None, ["COL", "PC"], ["MG"])
-    ts(T.PC[:, 4:5], pg, 16.0, 15.0, Op.mult, Op.add, ["PC"], ["PC3"])
-    diagonal("ID", 1.0)
-    diagonal("NI", -1.0)
-    diagonal("NS", -EPS)
-    ts(T.KP[0:32, :], T.KA[0:32, :], 1.0 / (4096 * 32), None, Op.mult, None, ["KA"], ["KP"])
+    scaled("IE", "ID", 1 + EPS)
+    scaled("NI", "ID", -1.0)
+    scaled("NS", "ID", -EPS)
+    scaled("KP", "KA", 1.0 / (4096 * 32), slice(0, 32))
     weights = [
         lambda: cp(T.WF[:], T.WT[:], ["WT"], ["WF"]),
         lambda: ts(T.WG[:], T.K2[:], T.WF[:, 1:2], T.WF[:, 0:1], Op.mult, Op.add, ["K2", "WF"], ["WG"]),
@@ -221,9 +228,6 @@ def rank_program(g, core, T, topo):
     ]
 
     def test_constants():
-        ts(T.BP[:], T.COL[:], T.PC[:, 4:5], BIG, Op.is_equal, Op.mult, ["COL", "PC3"], ["BP"])
-        ts(T.BN[:], T.COL[:], T.PC[:, 4:5], -BIG, Op.is_equal, Op.mult, ["COL", "PC3"], ["BN"])
-        ts(T.KQ[0:32, :], T.KB[0:32, :], 1.0 / 32, None, Op.mult, None, ["KB"], ["KQ"])
         ts(T.THR[:], T.L16[:], -BLOCK / 16, 7.0 * BLOCK + 32 * 4096, Op.mult, Op.add, ["L16"], ["THR"])
         ts(T.R1[:], T.L16[:], pl, float(OWN), Op.add, Op.add, ["L16", "PC"], ["R1"])
         ts(T.RSD[:, 0:128:16], T.L16[:], pl, float(SPARE), Op.add, Op.add, ["L16", "PC", "RSD"], ["RSD"])
@@ -235,8 +239,8 @@ def rank_program(g, core, T, topo):
     def compose_constants():
         for name, c in (("IS", EPS), ("I4", 1.0), ("N4", -1.0)):
             act(T[name][:], T.ID[:], Act.Identity, ["ID"], [name], scale=c)
-        act(T.T1[:], T.COLL[:], Act.Abs, ["COLL", "PC"], ["T1"], bias=pl, scale=-1.0)
-        act(T.CM[:], T.T1[:], Act.Identity, ["T1"], ["CM"], bias=4096.0, scale=61440.0)
+        act(T.COLL[:], T.COLL[:], Act.Abs, ["COLL", "PC"], ["COLL"], bias=pl, scale=-1.0)
+        act(T.CM[:], T.COLL[:], Act.Identity, ["COLL"], ["CM"], bias=4096.0, scale=61440.0)
         select("BLK", "BLK", [[16, 8], [0, 16]], Op.is_ge, 0.0, 15, -1)
         select("BLK", "BLK", [[-16, 8], [0, 16]], Op.is_ge, 0.0, 0, 1)
         select("TRI", "BLK", [[1, 128]], Op.is_gt, 0.0, 0, -1)
@@ -267,11 +271,11 @@ def rank_program(g, core, T, topo):
     def repeat(t, h):
         nm = ["pN", "pK"][h]
         for j in range(8):
-            mm(T[nm][:, :, j, :], T.ID[:], T["S%d" % t][:, 64 * h:64 * h + 64], True, True, ["ID", "S%d" % t], [nm])
+            mm(T[nm][:, :, j, :], T.IE[:], T["S%d" % t][:, 64 * h:64 * h + 64], True, True, ["IE", "S%d" % t], [nm])
 
     def addend(h):
         nm = ["pN", "pK"][h]
-        act(T.B[:, 512 * h:512 * h + 512], T[nm][:], Act.Identity, [nm], ["B%d" % h], bias=CH, scale=1 + EPS)
+        act(T.B[:, 512 * h:512 * h + 512], T[nm][:], Act.Identity, [nm], ["B%d" % h], bias=CH)
 
     EIGHTS = dict(pX=(0, 4), pF=(0, 1), pY=(1, 4))
 
@@ -322,7 +326,7 @@ def rank_program(g, core, T, topo):
         for j in range(16):
             mm(out, T[wt][:, 15 - j:143 - j], buf[:, c0 + j:c0 + 1024:16], False, stop and j == 15, r + [wt], [nm])
 
-    def tests(t):
+    def tests(t, before):
         def probe(c0, c1, add, r, w):
             x, o = ("XA%d" % t, 0) if c0 < 1024 else ("XB%d" % t, 64)
             tt(T.PHI[:, c0:c1], T.A[:, 0:W].indirect(T[x][:, c0 // 16 - o:c1 // 16 - o]), add, Op.add, At + [x] + r, [w])
@@ -331,69 +335,85 @@ def rank_program(g, core, T, topo):
             act(T.H[:, 1024 * q:1024 * q + 1024], T.PHI[:, 1024 * q:1024 * q + 1024], Act.Identity, PH[q], ["H%d" % q], bias=256.3)
             sums(T.pE[:, 64 * q:64 * q + 64], "pE", "BP", T.H, 1024 * q, ["H%d" % q], q == 2)
 
-        PH = [["PHa", "PH0"], ["PH1"], ["PH2"], ["PH3"]]
+        PH = [["PHa", "PH0"], ["PHc", "PH1"], ["PH2"], ["PHb", "PH3"]]
         probe(0, 512, T.B[:, 0:512], ["B0"], "PHa")
-        if t > 0:
-            addend(1)
         probe(512, 1024, T.B[:, 512:1024], ["B1"], "PH0")
-        for q in range(1, 4):
-            probe(1024 * q, 1024 * q + 1024, T.B[:], ["B0", "B1"], "PH%d" % q)
         keys(t)
-        if 1 <= t <= 3:
-            places(t - 1)
-        if t >= 1:
-            numbers(t - 1, T.PU[:, 8:16])
+        if RAW:
+            act(T.RW[:], T.A[:, 0:W].indirect(T["XB%d" % t][:, 0:32]), Act.Identity, At + ["XB%d" % t], ["RW"], bias=CH)
+            probe(1536, 2048, T.B[:, 512:1024], ["B1"], "PHc")
+            tt(T.PHI[:, 1024:1536], T.pN[:], T.RW[:], Op.add, ["pN", "RW"], ["PH1"])
+        else:
+            probe(1024, 2048, T.B[:], ["B0", "B1"], "PH1")
+        probe(2048, 3072, T.B[:], ["B0", "B1"], "PH2")
+        probe(3072, 3584, T.B[:, 0:512], ["B0"], "PHb")
+        probe(3584, 4096, T.B[:, 512:1024], ["B1"], "PH3")
         mm(T.pE[:, 0:192], T.ONE[0:32, :], T.KE[0:32, :], True, False, ["ONE", "KE"], ["pE"])
         mm(T.pF[:, 0:64], T.ONE[0:32, :], T.KE[0:32, 0:64], True, False, ["ONE", "KE"], ["pF"])
         if t == 0:
             act(T.D2[:, 0:ST], T.DR[:, 0:ST], Act.Identity, ["DR"], ["D2"], scale=2.0)
-            act(T.ND[:, 0:ST], T.DR[:, 0:ST], Act.Identity, ["DR"], ["ND"], scale=-1.0)
+            act(T.D2[:, 8:8 + ST], T.DR[:, 0:ST], Act.Identity, ["DR"], ["ND"], scale=-1.0)
             compose_constants()
         for q in range(3):
             sums(T.pE[:, 64 * q:64 * q + 64], "pE", "BN", T.PHI, 1024 * q, PH[q])
             halves(q)
-            if q == 1:
-                drift(t)
-        sums(T.pF[:, 0:64], "pF", "BN", T.PHI, 3072, ["PH3"])
-        act(T.H[:, 3072:3072 + HS], T.PHI[:, 3072:3072 + HS], Act.Identity, ["PH3"], ["H3s"], bias=256.3)
-        ts(T.H[:, 3072 + HS:4096], T.PHI[:, 3072 + HS:4096], 256.3, None, Op.add, None, ["PH3"], ["H3v"])
-        sums(T.pF[:, 0:64], "pF", "BP", T.H, 3072, ["H3s", "H3v"], True)
+        sums(T.pF[:, 0:64], "pF", "BN", T.PHI, 3072, PH[3])
+        act(T.H[:, 3072:3584], T.PHI[:, 3072:3584], Act.Identity, ["PHb"], ["H3a"], bias=256.3)
+        act(T.H[:, 3584:3584 + HS], T.PHI[:, 3584:3584 + HS], Act.Identity, ["PH3"], ["H3s"], bias=256.3)
+        drift(t)
+        if 1 <= t <= 3:
+            places(t - 1)
+        if t >= 1:
+            numbers(t - 1, T.PU[:, 8:16])
+        for f in before:
+            f()
+        if HS < 512:
+            ts(T.H[:, 3584 + HS:4096], T.PHI[:, 3584 + HS:4096], 256.3, None, Op.add, None, ["PH3"], ["H3v"])
+        sums(T.pF[:, 0:64], "pF", "BP", T.H, 3072, ["H3a", "H3s", "H3v"], True)
+
+    def effects(t, i):
+        a0, a1 = EFP[i]
+        if t >= 2 and a1 > a0:
+            tt(T.EF[:, 0:OWN].indirect(T.OU[:, a0:a1]), T["SN%d" % (t - 1)][:, 16 * a0:16 * a1],
+               T.MS[:, 128 * (t - 2) + 16 * a0:128 * (t - 2) + 16 * a1], Op.add,
+               ["SN%d" % (t - 1), "MS%d" % (t - 2), "OU"], ["EF", "EFd"])
 
     def first_hit(t):
-        if t >= 2:
-            tt(T.EF[:, 0:TW].indirect(T.OU[:, 0:8]), T["SN%d" % (t - 1)][:], T.MS[:, 128 * (t - 2):128 * (t - 1)], Op.add,
-               ["SN%d" % (t - 1), "MS%d" % (t - 2), "OU"], EFr)
         for q in range(3):
             cs = slice(64 * q, 64 * q + 64)
             scan(T.Z[:, cs], T.pE[:, cs], T["KEY%d" % t][:, cs], BIG, Op.min, Op.max, ["pE", "KEY%d" % t], ["Z%d" % q])
+        effects(t, 1)
         tt(T.R2[:], T.Z[:, 7:128:8], T.Z[:, 135:256:8], Op.min, ["Z0", "Z1", "Z2", "Zn"], ["R2"])
+        effects(t, 2)
         tt(T.R1[:], T.R2[:, 0:8], T.R2[:, 8:16], Op.min, ["R2"], ["R1"])
         scan(T.ZD[:, 0:64], T.pF[:, 0:64], T["KEY%d" % t][:, 192:256], BIG, Op.min, Op.max, ["pF", "KEY%d" % t], ["ZD"])
-        tt(T["KI%d" % t][:], T.ZD[:, 7:64:8], T.R1[:], Op.min, ["ZD", "R1"], ["KI%d" % t])
+        effects(t, 3)
+        tt(T.KI[:], T.ZD[:, 7:64:8], T.R1[:], Op.min, ["ZD", "R1"], ["KI"])
 
     def drift(t):
         act(T.RR[:], T["S%d" % t][:], Act.Relu, ["S%d" % t, "D2"], ["RR"], bias=T.D2[:, t:t + 1], scale=-2.0)
-        act(T.EF[:, OWN:TW], T.RR[:], Act.Identity, ["RR", "ND"], ["EFx"], bias=T.ND[:, t:t + 1])
+        act(T.EF[:, OWN:TW], T.RR[:], Act.Identity, ["RR", "ND"], ["EFx"], bias=T.D2[:, 8 + t:9 + t])
 
     def numbers(t, o):
         act(T.YP[:, 128 * t:128 * t + 128], T.COL[:, 0:64].indirect(o), Act.Copy, ["COL", "PU", "CU"], ["YP%d" % t])
 
     def place(t):
-        ki, kn = T["KI%d" % t][:], "KI%d" % t
-        number = lambda: ts(T.CK[:, 8:16], ki, 12, 63, Op.arith_shift_right, Op.bitwise_and, [kn], ["KK"])
+        ki, kn = T.KI[:], "KI"
+        pk, kk = T.CK[:, 0:8], T.CK[:, 8:16]
+        number = lambda: ts(kk, ki, 12, 63, Op.arith_shift_right, Op.bitwise_and, [kn], ["KK"])
         if t > 2:
-            return [number, lambda: cp(T.PU[:, 8:16], T.CK[:, 8:16], ["KK"], ["PU"])]
+            return [number, lambda: cp(T.PU[:, 8:16], kk, ["KK"], ["PU"])]
         return [
             lambda: tt(T.VD[:], T["KEY%d" % t][:, 198:256:8], T["KEY%d" % t][:, 199:256:8], Op.subtract, ["KEY%d" % t], ["VD"]),
             number,
-            lambda: ts(T.FL[:], T.CK[:, 8:16], 1.0, None, Op.is_ge, None, ["KK"], ["FL"]),
+            lambda: ts(T.FL[:], kk, 1.0, None, Op.is_ge, None, ["KK"], ["FL"]),
             lambda: tt(T.M1[:], T.FL[:], T.VD[:], Op.mult, ["FL", "VD"], ["M1"]),
-            lambda: tt(T.KN[:], ki, T.THR[:], Op.subtract, [kn, "THR"], ["KN"]),
+            lambda: tt(T.KM[:], ki, T.THR[:], Op.subtract, [kn, "THR"], ["KM"]),
             lambda: tt(T.P1[:], ki, T.M1[:], Op.subtract, [kn, "M1"], ["P1"]),
             lambda: ts(T.PL[:], T.P1[:], W - 1, None, Op.bitwise_and, None, ["P1"], ["PL"]),
-            lambda: tt(T.CK[:, 0:8], T.PL[:], T.KN[:], Op.max, ["PL", "KN"], ["PK"]),
+            lambda: tt(pk, T.PL[:], T.KM[:], Op.max, ["PL", "KM"], ["PK"]),
             lambda: cp(T.PU[:], T.CK[:], ["PK", "KK"], ["PU"]),
-            lambda: tt(T.PLT[:, 8 * t:8 * t + 8], T.CK[:, 0:8], T.THR[:], Op.add, ["PK", "THR"], ["PLT%d" % t])]
+            lambda: cp(T.PF[:, 8 * t:8 * t + 8], pk, ["PK"], ["PF%d" % t])]
 
     def places(t):
         act(T.PB[:, 128 * t:128 * t + 128], T.NUM[:, 0:TW].indirect(T.PU[:, 0:8]), Act.Copy, ["NUM", "NUMx", "PU"], ["PB%d" % t])
@@ -417,37 +437,54 @@ def rank_program(g, core, T, topo):
                                     (T["S%d" % k][:], "S%d" % k))):
             mm(out, T[ws[i]][:], x, i == 0, False, [ws[i], r], [nm])
 
-    def asked(t, a):
+    def apart(t):
         k = t - 1
-        ts(T.E[:, EO[a]:EO[a] + EW[a]], T.PB[:, 128 * k + 16 * a:128 * k + 128], float((7 - a) * BLOCK + 32 * 4096),
-           T.AP[:, a:a + 1], Op.add, Op.is_equal, ["PB%d" % k, "AP"], ["E%d" % a])
-        if a < 7:
-            mm(T.pD[:, 16 * a + 16:128], T.BLK[:], T.E[:, EO[a] + 16:EO[a] + EW[a]], False, False, ["BLK", "E%d" % a], ["pD"])
-        mm(T.pD[:, 16 * a:16 * a + 16], T.TRI[:], T.E[:, EO[a]:EO[a] + 16], False, a == 7, ["TRI", "E%d" % a], ["pD"])
+        for a in range(EV, 8):
+            act(T.EA[:, a, 0:128 - 16 * a], T.PB[:, 128 * k + 16 * a:128 * k + 128], Act.Abs, ["PB%d" % k, "PF%d" % k], ["EA%d" % a],
+                bias=T.PF[:, 8 * k + a:8 * k + a + 1], scale=-1.0)
 
-    blocks("S0", range(NG), "s")
-    for f in weights:
-        f()
+    def asked(t, a, last):
+        k = t - 1
+        if a < EV:
+            ts(T.E[:, a, 0:128 - 16 * a], T.PB[:, 128 * k + 16 * a:128 * k + 128], T.PF[:, 8 * k + a:8 * k + a + 1],
+               T["FN%d" % t][:, a:a + 1], Op.is_equal, Op.mult, ["PB%d" % k, "PF%d" % k, "FN%d" % t], ["E%d" % a])
+        else:
+            act(T.E[:, a, 0:128 - 16 * a], T.EA[:, a, 0:128 - 16 * a], Act.Relu, ["EA%d" % a, "FN%d" % t], ["E%d" % a],
+                bias=T["FN%d" % t][:, a:a + 1], scale=-1.0)
+        if a < 7:
+            mm(T.pD[:, 16 * a + 16:128], T.BLK[:], T.E[:, a, 16:128 - 16 * a], False, False, ["BLK", "E%d" % a], ["pD"])
+        if a in (EV - 1, 7):
+            b0, b1 = (EV, 8) if a == 7 else (0, EV)
+            mm(T.pD[:, 16 * b0:16 * b1], T.TRI[:], T.E[:, b0:b1, 0:16], False, last, ["TRI"] + ["E%d" % b for b in range(b0, b1)], ["pD"])
+
+    for k in range(5):
+        weights[k]()
+        blocks("S0", [k], "v")
+    blocks("S0", range(5, 8), "s")
     send(prv, "WN", T.WH[:], ["WH"])
     repeat(0, 0)
     addend(0)
     repeat(0, 1)
     for nm in EIGHTS:
         begin(nm)
+    for nm in EIGHTS:
         linear(nm, "WH", nm == "pX")
     addend(1)
+    ms(T.NUM[:, W:TW], 4094.0, ["NUMx"])
     for nm in ("pF", "pY"):
         whole_part(nm)
-        remainder(nm)
     test_constants()
     for nm in ("pF", "pY"):
+        remainder(nm)
         offsets(nm, 0)
     for k in range(len(PACKS)):
         pack(k)
+    scaled("BN", "BP", -1.0)
+    scaled("KQ", "KB", 1.0 / 32, slice(0, 32))
 
     for t in range(ST):
         s_, St = "S%d" % t, T["S%d" % t]
-        tests(t)
+        tests(t, [lambda: effects(t, 0)])
         if t == ST - 1:
             dma("y", T.yp[:, 0:512], T.YP[0:128:16, 0:512], ["YP%d" % k for k in range(4)], [], "d_yp0")
         if 1 <= t <= 3:
@@ -462,11 +499,14 @@ def rank_program(g, core, T, topo):
             if later:
                 later.pop(0)()
 
-        ki, kn = T["KI%d" % t][:], "KI%d" % t
-        if 1 <= t <= 3:
-            send(prv, "KN%d" % t, ki, [kn])
+        ki, kn = T.KI[:], "KI"
         fill()
         ts(T.CI[:, 0:8], ki, 4095, None, Op.bitwise_and, None, [kn], ["CI"])
+        if 1 <= t <= 3:
+            tt(T.FA[:, t - 1], ki, T.THR[:], Op.is_lt, [kn, "THR"], ["FA%d" % t])
+            send(prv, "FN%d" % t, T.FA[:, t - 1], ["FA%d" % t])
+        else:
+            fill()
         col = T.CU[:, 0:8]
         if t == ST - 1:
             ts(T.CI[:, 8:16], ki, 12, 63, Op.arith_shift_right, Op.bitwise_and, [kn], ["KK"])
@@ -476,7 +516,6 @@ def rank_program(g, core, T, topo):
             numbers(t, T.CU[:, 8:16])
             dma("s", T.yp[:, 512:640], T.YP[0:128:16, 512:640], ["YP4"], [], "d_yp1")
             break
-        fill()
         cp(col, T.CI[:, 0:8], ["CI"], ["CU"])
         fill()
         so, So, Gt = "SO%d" % t, T["SO%d" % t], T["G%d" % t][:]
@@ -485,12 +524,19 @@ def rank_program(g, core, T, topo):
         if t == 0:
             send(nxt, "S1", So[:], [so])
         else:
-            send_together([(nxt, "S%d" % (t + 1), So, [so], 1), (prv, "GN%d" % t, T["G%d" % t], ["G%d" % t], 2)])
+            send(prv, "GN%d" % t, Gt, ["G%d" % t])
+            send_together([(nxt, "S%d" % (t + 1), So, [so], 1), (prv, "SN%d" % t, So, [so], 1)])
         gn, ga = "GN%d" % t, "G%d" % (t - 1)
-        blocks_left = list(range(8))
+        left = [list(range(EV)), list(range(EV, 8))]
+
+        def compare(i):
+            a = left[i].pop(0)
+            asked(t, a, not left[0] + left[1])
+
         forward = dict(
             masks_s=lambda: blocks(so, range(0, NS_), "s"), masks_v=lambda: blocks(so, range(NS_, NG), "v"),
             repeat0=lambda: repeat(t + 1, 0), repeat1=lambda: repeat(t + 1, 1), addend=lambda: addend(0),
+            addend1=lambda: addend(1),
             probes=lambda: linear("pX", "WN", True),
             again_a=lambda: linear("pF", "WN", False), again_b=lambda: linear("pY", "WN", False),
             whole_a=lambda: whole_part("pF"), whole_b=lambda: whole_part("pY"),
@@ -499,9 +545,8 @@ def rank_program(g, core, T, topo):
             fill=fill, kept=lambda: kept(t) if t <= 2 else None)
         back = dict(
             w_open=lambda: open_sum(t, "pE", T.pE[:, 256:384], ["N4", "ID", "IS", "NS"]),
-            states=lambda: send(prv, "SN%d" % t, So[:], [so]),
-            ask=lambda: tt(T.AP[:], T["KN%d" % t][:], T.PLT[:, 8 * t - 8:8 * t], Op.max, ["KN%d" % t, "PLT%d" % (t - 1)], ["AP"]),
-            e=lambda: asked(t, blocks_left.pop(0)),
+            apart=lambda: apart(t),
+            e=lambda: compare(0), es=lambda: compare(1),
             lows=lambda: act(T.NB[:], T[gn][:], Act.Identity, [gn], ["NB"], bias=1280.0),
             w_bounds=lambda: mm(T.pE[:, 256:384], T.I4[:], T[gn][:], False, False, ["I4", gn], ["pE"]),
             u_lows=lambda: mm(T.pU[:, 0:128], T.ID[:], T.NB[:], False, True, ["ID", "NB"], ["pU"]),
@@ -511,7 +556,7 @@ def rank_program(g, core, T, topo):
             lowest=lambda: scan(T.ZD[:], T.RSD[:], T.pD[:, 0:128], 0.0, Op.max, Op.min, ["RSD", "pD"], ["ZD"]),
             served=lambda: cp(T.OU[:], T.ZD[:, 15:128:16], ["ZD"], ["OU"]),
             scatter=lambda: tt(T.A[:, 0:TW].indirect(T.OU[:, 0:8]), T.U[:], T.UW[:], Op.add, ["U", "UW", "OU"], At))
-        for name in ORDER.split():
+        for name in ORDER.split("|")[0 if near(nxt) else 1].split():
             if name in forward:
                 forward[name]()
             elif t >= 1:

from concourse.bass import DstId, RemoteDMATransfer
from concourse.mybir import AluOpType as Op, ActivationFunctionType as Act

W, L, ST = 2048, 128, 5
SPARE, OWN, TW = 2048, 2176, 2304
EPS = 1.0 / 1024
CH = 768.25 - EPS / 2
HS = 256
BIG = float(2 ** 23)
MAGIC = 1.5 * 2 ** 23
BLOCK = 2 ** 18
NG, NS_ = 8, 3
EV = 3
RAW = True
ORDER = ("w_open fill masks_v masks_s apart probes fill again_a e e whole_a rest_a again_b fill e es es es es es whole_b lows "
         "u_lows rest_b w_bounds w_lows w offsets_a repeat0 addend fill lowest offsets_b fill served u fill repeat1 scatter addend1 "
         "kept |"
         "w_open fill masks_v fill masks_s apart probes fill whole_a again_a rest_a again_b fill whole_b offsets_a es es rest_b e e "
         "es es es e lows w_bounds u_lows w_lows offsets_b repeat0 lowest w fill repeat1 served addend addend1 u fill scatter kept")
EFP = [(0, 2), (2, 6), (6, 8), (8, 8)]
LOADS = [(0, 1024), (1024, 1792), (1792, 2048)]
PACKS = [(0, 512), (512, 1024), (1024, 1408), (1408, 1792), (1792, 1920), (1920, 2048)]
F32, BF, F16, I32, U16 = "float32", "bfloat16", "float16", "int32", "uint16"
SCRATCH = {}
for _d, _names in (
        (F32, dict(A=TW, NUM=TW, WF=2, D2=16, WG=32, PC=5, COL=144, COLL=128, K2=32, KA=256, KB=256, L16=8, THR=8,
                   MG=8, RSD=128, I4=128, N4=128, PF=24, B=1024, Z=264, R2=16, R1=8, FL=8, VD=8,
                   M1=8, RW=512, ZD=128, U=128, UW=128, YS=128, YP=640)),
        (BF, dict(LO=W, HI=W, EF=TW, DR=8, KE=192, ONE=128, CM=128, ID=128, NI=128, IS=128, NS=128, BLK=128,
                  TRI=128, BP=144, BN=144, RR=128, MS=384)),
        (F16, dict(WH=32, WN=32, IE=128, KP=256, KQ=256, RD=256, PHI=4096, H=4096, NA=384, NB=128, PB=384)),
        (I32, dict(WT=2, WI=32, WJ=32, PI=4, CI=16, P1=8, PL=8, CK=16, KM=8, KI=8)),
        (U16, dict(CU=16, PU=16, OU=8))):
    for _k, _n in _names.items():
        SCRATCH[_k] = ("sbuf", [128, _n], _d)
SCRATCH["SM"] = ("sbuf", [128, 8, 8, 16], BF)
SCRATCH["FA"] = ("sbuf", [128, 3, 8], F32)
SCRATCH["E"] = ("sbuf", [128, 8, 128], BF)
SCRATCH["EA"] = ("sbuf", [128, 8, 128], F32)
for _k, _s in dict(pX=[8, 8, 8], pN=[4, 8, 16], pK=[4, 8, 16], pE=[512], pF=[512], pD=[512], pU=[512], pY=[8, 8, 8]).items():
    SCRATCH[_k] = ("psum", [128] + _s, F32)
for _k, _ts, _n, _d in (("S", range(5), 128, BF),
                        ("SO", range(4), 128, BF),
                        ("XA", range(5), 64, U16),
                        ("XB", range(5), 192, U16),
                        ("KEY", range(5), 256, F32),
                        ("G", range(4), 128, F32),
                        ("FN", range(1, 4), 8, F32),
                        ("GN", range(1, 4), 128, F32),
                        ("SN", range(1, 4), 128, BF)):
    for _t in _ts:
        SCRATCH["%s%d" % (_k, _t)] = ("sbuf", [128, _n], _d)

for _k in ("XA", "XB", "KEY"):
    SCRATCH["O" + _k] = ("sbuf", [128, 4, SCRATCH[_k + "0"][1][1]], SCRATCH[_k + "0"][2])
SEMAPHORES = (["qg", "qv", "qs", "qp", "sent", "d_s0", "d_wt", "d_dr", "d_ef", "d_ys", "d_yp0", "d_yp1"]
              + ["d_%s%d" % (x, k) for x in ("lo", "hi") for k in range(len(LOADS))]
              + ["r_WN"] + ["r_%s%d" % (k, t) for k in ("S", "XA", "XB", "KEY") for t in range(1, 5)]
              + ["r_%s%d" % (k, t) for k in ("FN", "GN", "SN") for t in range(1, 4)])


def rank_program(g, core, T, topo):
    rank = T.rank_of(core)
    if rank is None:
        return
    n = len(T.cores)
    nxt, prv = T.cores[(rank + 1) % n], T.cores[(rank - 1) % n]

    Q = {"g": g, "v": g.vector, "s": g.scalar, "p": g.tensor, "y": g.sync}
    seen = {q: {} for q in Q}
    total, clock, wrote, read = {}, {}, {}, {}

    def wait(q, toks):
        best = {}
        for s, v in toks:
            if not (q == "p" and s == "qp"):
                best[s] = max(best.get(s, 0), v)
        for s, v in sorted(best.items(), key=lambda e: -len(clock.get(e, {}))):
            if seen[q].get(s, 0) < v:
                Q[q].wait_ge(T.sem[s], v)
                seen[q][s] = v
                for s2, v2 in clock.get((s, v), {}).items():
                    if seen[q].get(s2, 0) < v2:
                        seen[q][s2] = v2

    def op(q, fn, r, w, sem=None, inc=1):
        toks = []
        for x in r:
            toks += wrote.get(x, [])
            if x[0] == "p":
                toks += [k for k in read.get(x, []) if k[0] != "q" + q]
        for x in w:
            toks += wrote.get(x, []) + read.get(x, [])
        wait(q, toks)
        s = sem or "q" + q
        fn().then_inc(T.sem[s], inc)
        total[s] = total.get(s, 0) + inc
        tok = (s, total[s])
        clock[tok] = dict(seen[q])
        for x in r:
            read.setdefault(x, []).append(tok)
        for x in w:
            wrote[x], read[x] = [tok], []

    def dma(q, out, in_, r, w, sem):
        op(q, lambda: Q[q].dma_start(out, in_), r, w, sem, 16)

    def near(c):
        return c in topo.cores_of(core)

    def engines(src, dst, name=""):
        far = topo.mask(src, [c for c in T.cores if c not in topo.cores_of(src)][0])
        if name == "WN":
            return topo.mask(src, dst)
        return far if name in ("S1", "XA1", "XB1") else topo.mask(src, dst) & ~far or far

    def send(dst, name, in_, r):
        mask = engines(core, dst, name)
        wait("g", [k for x in r for k in wrote.get(x, [])])
        rid, pid = topo.addr(dst, core)
        g.remote_dma(T[name][:], in_, T.sem["r_" + name], T.sem["sent"], pid, rid, mask)
        total["sent"] = total.get("sent", 0) + bin(mask).count("1")

    def send_together(msgs):
        transfers = []
        for dst, name, in_, r, pieces in msgs:
            wait("g", [k for x in r for k in wrote.get(x, [])])
            rid, pid = topo.addr(dst, core)
            es = [e for e in topo.engines(core, dst) if engines(core, dst) >> e & 1]
            wd, ne = in_.shape[1] // pieces, len(es) // pieces
            for i in range(pieces):
                transfers.append(RemoteDMATransfer(
                    dst_ids=[DstId(rid=rid, pnc=pid)], dma_engine_mask=sum(1 << e for e in es[ne * i:ne * i + ne]),
                    remote_sem=T.sem["r_" + name], src=in_[:, wd * i:wd * i + wd], dst=T[name][:, wd * i:wd * i + wd]))
            total["sent"] = total.get("sent", 0) + len(es)
        g.remote_dma_fused(transfers, local_sem=T.sem["sent"])

    def lands(name, src):
        k = bin(engines(src, core, name)).count("1")
        wrote[name], total["r_" + name] = [("r_" + name, k)], k

    V, S, P = g.vector, g.scalar, g.tensor

    def ts(out, in0, s1, s2, o0, o1, r, w):
        if o1 is None:
            op("v", lambda: V.tensor_scalar(out, in0, s1, None, o0), r, w)
        else:
            op("v", lambda: V.tensor_scalar(out, in0, s1, s2, o0, o1), r, w)

    def tt(out, a, b, o, r, w):
        op("v", lambda: V.tensor_tensor(out, a, b, o), r, w)

    def cp(out, a, r, w):
        op("v", lambda: V.tensor_copy(out, a), r, w)

    def ms(out, c, w):
        op("v", lambda: V.memset(out, c), [], w)

    def scan(out, d0, d1, first, o0, o1, r, w):
        op("v", lambda: V.tensor_tensor_scan(out, d0, d1, first, o0, o1), r, w)

    def act(out, a, f, r, w, bias=0.0, scale=1.0):
        op("s", lambda: S.activation(out, a, f, bias=bias, scale=scale), r, w)

    def mm(out, lt, rh, st, sp, r, w):
        op("p", lambda: P.matmul(out, lt, rh, st, sp), r, w)

    def iota(out, pat, base, cm, w, whole=False):
        if whole:
            op("g", lambda: g.iota(out, pat, base, cm), [], w)
        else:
            op("g", lambda: g.iota(out, pat, base, cm, allow_small_or_imprecise_dtypes=True), [], w)

    lands("WN", nxt)
    for t in range(1, 5):
        for k in ("S", "XA", "XB", "KEY"):
            lands("%s%d" % (k, t), prv)
    for t in range(1, 4):
        for k in ("FN", "GN", "SN"):
            lands("%s%d" % (k, t), nxt)

    dma("y", T.S0[:], T.s0[:], [], ["S0"], "d_s0")
    dma("s", T.WT[:], T.wt[:], [], ["WT"], "d_wt")
    for h, (c0, c1) in enumerate(LOADS):
        cs = slice(c0, c1)
        dma("y", T.LO[:, cs], T.lo[:, cs], [], ["LO%d" % h], "d_lo%d" % h)
        dma("s", T.HI[:, cs], T.hi[:, cs], [], ["HI%d" % h], "d_hi%d" % h)
    last = "HI%d" % (len(LOADS) - 1)
    dma("y", T.DR[:, 0:ST], T.dr[:], [last], ["DR"], "d_dr")
    dma("y", T.EF[:, 0:W], T.ef[:], [last], ["EF"], "d_ef")

    iota(T.PI[:, 0:1], [[0, 1]], 0, 1, ["PI0"], True)
    iota(T.COL[:], [[1, 144]], 0, 0, ["COL"])
    iota(T.K2[:], [[-2, 32]], 62, 0, ["K2"])
    iota(T.KA[0:32, :], [[-16, 4], [0, 8], [-2, 8]], 63 - W, 0, ["KA"])
    iota(T.KB[0:32, :], [[-16, 4], [-BLOCK // W, 8], [-2, 8]], 62 + 7 * BLOCK // W, 0, ["KB"])
    iota(T.L16[:], [[16, 8]], 0, 0, ["L16"])
    iota(T.COLL[:], [[0, 8], [1, 16]], 0, 0, ["COLL"])
    iota(T.NUM[:, 0:W], [[1, W]], 0, 0, ["NUM"])
    ms(T.ONE[0:32, :], 1.0, ["ONE"])
    ms(T.KE[0:32, :], -BIG * 128, ["KE"])
    ts(T.PI[:, 1:2], T.PI[:, 0:1], 15, None, Op.bitwise_and, None, ["PI0"], ["PI1"])
    ts(T.PI[:, 2:3], T.PI[:, 0:1], 4, None, Op.arith_shift_right, None, ["PI0"], ["PI2"])
    ms(T.RSD[:], 0.0, ["RSD"])
    cp(T.PC[:, 0:3], T.PI[:, 0:3], ["PI0", "PI1", "PI2"], ["PC"])
    ms(T.BLK[:], 4096.0, ["BLK"])
    ms(T.EF[:, SPARE:OWN], 0.0, ["EFd"])
    pp, pl, pg = T.PC[:, 0:1], T.PC[:, 1:2], T.PC[:, 2:3]
    ts(T.ID[:], T.COL[:, 0:128], pp, None, Op.is_equal, None, ["COL", "PC"], ["ID"])
    ts(T.MG[:], T.COL[:, 0:8], pg, None, Op.is_equal, None, ["COL", "PC"], ["MG"])
    ts(T.PC[:, 3:4], pg, 16.0, 15.0, Op.mult, Op.add, ["PC"], ["PC3"])
    ms(T.A[:, W:TW], 0.0, ["Ax"])
    ts(T.BP[:], T.COL[:], T.PC[:, 3:4], BIG, Op.is_equal, Op.mult, ["COL", "PC3"], ["BP"])

    def scaled(out, in_, c, ps=slice(0, 128)):
        act(T[out][ps, :], T[in_][ps, :], Act.Identity, [in_], [out], scale=c)

    scaled("IE", "ID", 1 + EPS)
    scaled("NI", "ID", -1.0)
    scaled("NS", "ID", -EPS)
    scaled("KP", "KA", 1.0 / (4096 * 32), slice(0, 32))
    weights = [
        lambda: cp(T.WF[:], T.WT[:], ["WT"], ["WF"]),
        lambda: ts(T.WG[:], T.K2[:], T.WF[:, 1:2], T.WF[:, 0:1], Op.mult, Op.add, ["K2", "WF"], ["WG"]),
        lambda: ts(T.WI[:], T.WG[:], W / 2, None, Op.add, None, ["WG"], ["WI"]),
        lambda: ts(T.WJ[:], T.WI[:], W - 1, None, Op.bitwise_and, None, ["WI"], ["WJ"]),
        lambda: ts(T.WH[:], T.WJ[:], -W / 2, 1.0 / W, Op.add, Op.mult, ["WJ"], ["WH"]),
    ]

    def test_constants():
        ts(T.THR[:], T.L16[:], -BLOCK / 16, 7.0 * BLOCK + 32 * 4096, Op.mult, Op.add, ["L16"], ["THR"])
        ts(T.R1[:], T.L16[:], pl, float(OWN), Op.add, Op.add, ["L16", "PC"], ["R1"])
        ts(T.RSD[:, 0:128:16], T.L16[:], pl, float(SPARE), Op.add, Op.add, ["L16", "PC", "RSD"], ["RSD"])
        tt(T.Z[:, 199:256:8], T.R1[:], T.THR[:], Op.add, ["R1", "THR"], ["Zn"])

    def select(out, in_, pat, how, other, base, cm):
        op("g", lambda: g.affine_select(T[out][:], T[in_][:], pat, how, other, base, cm), [in_], [out])

    def compose_constants():
        for name, c in (("IS", EPS), ("I4", 1.0), ("N4", -1.0)):
            act(T[name][:], T.ID[:], Act.Identity, ["ID"], [name], scale=c)
        act(T.COLL[:], T.COLL[:], Act.Abs, ["COLL", "PC"], ["COLL"], bias=pl, scale=-1.0)
        act(T.CM[:], T.COLL[:], Act.Identity, ["COLL"], ["CM"], bias=4096.0, scale=61440.0)
        select("BLK", "BLK", [[16, 8], [0, 16]], Op.is_ge, 0.0, 15, -1)
        select("BLK", "BLK", [[-16, 8], [0, 16]], Op.is_ge, 0.0, 0, 1)
        select("TRI", "BLK", [[1, 128]], Op.is_gt, 0.0, 0, -1)
        select("TRI", "TRI", [[1, 128]], Op.not_equal, -4096.0, 0, -1)

    At = ["A%d" % k for k in range(len(PACKS))] + ["Ax"]
    EFr = ["EF", "EFx", "EFd"]
    SMr = ["SM%d" % k for k in range(NG)]

    def pack(k):
        nm, (c0, c1) = ["pD", "pU", "pE", "pF"][k % 4], PACKS[k]
        h = [i for i in range(len(LOADS)) if LOADS[i][0] <= c0][-1]
        out = T[nm][:, 0:c1 - c0]
        mm(out, T.NI[:], T.LO[:, c0:c1], True, False, ["NI", "LO%d" % h], [nm])
        mm(out, T.NS[:], T.HI[:, c0:c1], False, True, ["NS", "HI%d" % h], [nm])
        if k % 2:
            cp(T.A[:, c0:c1], out, [nm], [At[k]])
        else:
            act(T.A[:, c0:c1], out, Act.Copy, [nm], [At[k]])

    def blocks(s, ks, q):
        for k in ks:
            if q == "v":
                ts(T.SM[:, :, k, :], T[s][:], T.MG[:, k:k + 1], None, Op.mult, None, [s, "MG"], [SMr[k]])
            else:
                act(T.SM[:, :, k, :], T[s][:], Act.Identity, [s, "MG"], [SMr[k]], scale=T.MG[:, k:k + 1])

    def repeat(t, h):
        nm = ["pN", "pK"][h]
        for j in range(8):
            mm(T[nm][:, :, j, :], T.IE[:], T["S%d" % t][:, 64 * h:64 * h + 64], True, True, ["IE", "S%d" % t], [nm])

    def addend(h):
        nm = ["pN", "pK"][h]
        act(T.B[:, 512 * h:512 * h + 512], T[nm][:], Act.Identity, [nm], ["B%d" % h], bias=CH)

    EIGHTS = dict(pX=(0, 4), pF=(0, 1), pY=(1, 4))

    def part(nm, a=None):
        q0, q1 = EIGHTS[nm]
        if nm == "pF":
            return T.pF[:, 0:64] if a is None else T.pF[:, 8 * a:8 * a + 8]
        return T[nm][:, q0:q1] if a is None else T[nm][:, q0:q1, a, :]

    def begin(nm, more=()):
        q0, q1 = EIGHTS[nm]
        for i, c in enumerate(("KP",) + more):
            mm(part(nm), T.ONE[0:32, :], T[c][0:32, 64 * q0:64 * q1], i == 0, False, ["ONE", c], [nm])

    def linear(nm, w, stop):
        q0, q1 = EIGHTS[nm]
        for a in range(8):
            mm(part(nm, a), T.SM[:, a], T[w][:, 8 * q0:8 * q1], False, stop and a == 7, SMr + [w], [nm])

    def whole_part(nm):
        q0, q1 = EIGHTS[nm]
        ts(T.RD[:, 64 * q0:64 * q1], T.pX[:, q0:q1], MAGIC, MAGIC, Op.add, Op.subtract, ["pX"], ["RD" + nm])

    def remainder(nm):
        q0, q1 = EIGHTS[nm]
        mm(part(nm), T.NI[:], T.RD[:, 64 * q0:64 * q1], False, True, ["NI"] + (["RDpF", "RDpY"] if nm == "pX" else ["RD" + nm]), [nm])

    def hand_on(name, t):
        return (name + "0", T[name + "0"][:]) if t == 0 else ("O%s%d" % (name, t), T["O" + name][:, t - 1])

    def offsets(nm, t):
        name = dict(pF="XA", pY="XB")[nm]
        out, ap = hand_on(name, t)
        ts(ap, part(nm), float(W), W / 2 - 0.5, Op.mult, Op.add, [nm], [out])
        if t > 0:
            send(nxt, "%s%d" % (name, t), ap, [out])

    def keys(t):
        begin("pX", ("KQ",))
        linear("pX", "WN" if t else "WH", False)
        remainder("pX")
        out, ap = hand_on("KEY", t)
        act(ap, T.pX[:, 0:4], Act.Identity, ["pX"], [out], bias=W / 2 - 0.5, scale=float(W))
        if t > 0:
            send(nxt, "KEY%d" % t, ap, [out])

    def sums(out, nm, wt, buf, c0, r, stop=False):
        for j in range(16):
            mm(out, T[wt][:, 15 - j:143 - j], buf[:, c0 + j:c0 + 1024:16], False, stop and j == 15, r + [wt], [nm])

    def tests(t, before):
        def probe(c0, c1, add, r, w):
            x, o = ("XA%d" % t, 0) if c0 < 1024 else ("XB%d" % t, 64)
            tt(T.PHI[:, c0:c1], T.A[:, 0:W].indirect(T[x][:, c0 // 16 - o:c1 // 16 - o]), add, Op.add, At + [x] + r, [w])

        def halves(q):
            act(T.H[:, 1024 * q:1024 * q + 1024], T.PHI[:, 1024 * q:1024 * q + 1024], Act.Identity, PH[q], ["H%d" % q], bias=256.3)
            sums(T.pE[:, 64 * q:64 * q + 64], "pE", "BP", T.H, 1024 * q, ["H%d" % q], q == 2)

        PH = [["PHa", "PH0"], ["PHc", "PH1"], ["PH2"], ["PHb", "PH3"]]
        probe(0, 512, T.B[:, 0:512], ["B0"], "PHa")
        probe(512, 1024, T.B[:, 512:1024], ["B1"], "PH0")
        keys(t)
        if RAW:
            act(T.RW[:], T.A[:, 0:W].indirect(T["XB%d" % t][:, 0:32]), Act.Identity, At + ["XB%d" % t], ["RW"], bias=CH)
            probe(1536, 2048, T.B[:, 512:1024], ["B1"], "PHc")
            tt(T.PHI[:, 1024:1536], T.pN[:], T.RW[:], Op.add, ["pN", "RW"], ["PH1"])
        else:
            probe(1024, 2048, T.B[:], ["B0", "B1"], "PH1")
        probe(2048, 3072, T.B[:], ["B0", "B1"], "PH2")
        probe(3072, 3584, T.B[:, 0:512], ["B0"], "PHb")
        probe(3584, 4096, T.B[:, 512:1024], ["B1"], "PH3")
        mm(T.pE[:, 0:192], T.ONE[0:32, :], T.KE[0:32, :], True, False, ["ONE", "KE"], ["pE"])
        mm(T.pF[:, 0:64], T.ONE[0:32, :], T.KE[0:32, 0:64], True, False, ["ONE", "KE"], ["pF"])
        if t == 0:
            act(T.D2[:, 0:ST], T.DR[:, 0:ST], Act.Identity, ["DR"], ["D2"], scale=2.0)
            act(T.D2[:, 8:8 + ST], T.DR[:, 0:ST], Act.Identity, ["DR"], ["ND"], scale=-1.0)
            compose_constants()
        for q in range(3):
            sums(T.pE[:, 64 * q:64 * q + 64], "pE", "BN", T.PHI, 1024 * q, PH[q])
            halves(q)
        sums(T.pF[:, 0:64], "pF", "BN", T.PHI, 3072, PH[3])
        act(T.H[:, 3072:3584], T.PHI[:, 3072:3584], Act.Identity, ["PHb"], ["H3a"], bias=256.3)
        act(T.H[:, 3584:3584 + HS], T.PHI[:, 3584:3584 + HS], Act.Identity, ["PH3"], ["H3s"], bias=256.3)
        drift(t)
        if 1 <= t <= 3:
            places(t - 1)
        if t >= 1:
            numbers(t - 1, T.PU[:, 8:16])
        for f in before:
            f()
        if HS < 512:
            ts(T.H[:, 3584 + HS:4096], T.PHI[:, 3584 + HS:4096], 256.3, None, Op.add, None, ["PH3"], ["H3v"])
        sums(T.pF[:, 0:64], "pF", "BP", T.H, 3072, ["H3a", "H3s", "H3v"], True)

    def effects(t, i):
        a0, a1 = EFP[i]
        if t >= 2 and a1 > a0:
            tt(T.EF[:, 0:OWN].indirect(T.OU[:, a0:a1]), T["SN%d" % (t - 1)][:, 16 * a0:16 * a1],
               T.MS[:, 128 * (t - 2) + 16 * a0:128 * (t - 2) + 16 * a1], Op.add,
               ["SN%d" % (t - 1), "MS%d" % (t - 2), "OU"], ["EF", "EFd"])

    def first_hit(t):
        for q in range(3):
            cs = slice(64 * q, 64 * q + 64)
            scan(T.Z[:, cs], T.pE[:, cs], T["KEY%d" % t][:, cs], BIG, Op.min, Op.max, ["pE", "KEY%d" % t], ["Z%d" % q])
        effects(t, 1)
        tt(T.R2[:], T.Z[:, 7:128:8], T.Z[:, 135:256:8], Op.min, ["Z0", "Z1", "Z2", "Zn"], ["R2"])
        effects(t, 2)
        tt(T.R1[:], T.R2[:, 0:8], T.R2[:, 8:16], Op.min, ["R2"], ["R1"])
        scan(T.ZD[:, 0:64], T.pF[:, 0:64], T["KEY%d" % t][:, 192:256], BIG, Op.min, Op.max, ["pF", "KEY%d" % t], ["ZD"])
        effects(t, 3)
        tt(T.KI[:], T.ZD[:, 7:64:8], T.R1[:], Op.min, ["ZD", "R1"], ["KI"])

    def drift(t):
        act(T.RR[:], T["S%d" % t][:], Act.Relu, ["S%d" % t, "D2"], ["RR"], bias=T.D2[:, t:t + 1], scale=-2.0)
        act(T.EF[:, OWN:TW], T.RR[:], Act.Identity, ["RR", "ND"], ["EFx"], bias=T.D2[:, 8 + t:9 + t])

    def numbers(t, o):
        act(T.YP[:, 128 * t:128 * t + 128], T.COL[:, 0:64].indirect(o), Act.Copy, ["COL", "PU", "CU"], ["YP%d" % t])

    def place(t):
        ki, kn = T.KI[:], "KI"
        pk, kk = T.CK[:, 0:8], T.CK[:, 8:16]
        number = lambda: ts(kk, ki, 12, 63, Op.arith_shift_right, Op.bitwise_and, [kn], ["KK"])
        if t > 2:
            return [number, lambda: cp(T.PU[:, 8:16], kk, ["KK"], ["PU"])]
        return [
            lambda: tt(T.VD[:], T["KEY%d" % t][:, 198:256:8], T["KEY%d" % t][:, 199:256:8], Op.subtract, ["KEY%d" % t], ["VD"]),
            number,
            lambda: ts(T.FL[:], kk, 1.0, None, Op.is_ge, None, ["KK"], ["FL"]),
            lambda: tt(T.M1[:], T.FL[:], T.VD[:], Op.mult, ["FL", "VD"], ["M1"]),
            lambda: tt(T.KM[:], ki, T.THR[:], Op.subtract, [kn, "THR"], ["KM"]),
            lambda: tt(T.P1[:], ki, T.M1[:], Op.subtract, [kn, "M1"], ["P1"]),
            lambda: ts(T.PL[:], T.P1[:], W - 1, None, Op.bitwise_and, None, ["P1"], ["PL"]),
            lambda: tt(pk, T.PL[:], T.KM[:], Op.max, ["PL", "KM"], ["PK"]),
            lambda: cp(T.PU[:], T.CK[:], ["PK", "KK"], ["PU"]),
            lambda: cp(T.PF[:, 8 * t:8 * t + 8], pk, ["PK"], ["PF%d" % t])]

    def places(t):
        act(T.PB[:, 128 * t:128 * t + 128], T.NUM[:, 0:TW].indirect(T.PU[:, 0:8]), Act.Copy, ["NUM", "NUMx", "PU"], ["PB%d" % t])

    def kept(t):
        cs = slice(128 * t, 128 * t + 128)
        act(T.NA[:, cs], T["G%d" % t][:], Act.Identity, ["G%d" % t], ["NA%d" % t], bias=1280.0)
        act(T.MS[:, cs], T["S%d" % t][:], Act.Identity, ["S%d" % t], ["MS%d" % t], scale=-1.0)

    def open_sums(t):
        k = t - 1
        cs = slice(128 * k, 128 * k + 128)
        mm(T.pD[:, 0:128], T.ID[:], T.PB[:, cs], True, False, ["ID", "PB%d" % k], ["pD"])
        mm(T.pD[:, 0:128], T.ID[:], T.CM[:], False, False, ["ID", "CM"], ["pD"])
        open_sum(t, "pU", T.pU[:, 0:128], ["I4", "NI", "ID", "NI"])

    def open_sum(t, nm, out, ws):
        k = t - 1
        cs = slice(128 * k, 128 * k + 128)
        for i, (x, r) in enumerate(((T["G%d" % k][:], "G%d" % k), (T.NA[:, cs], "NA%d" % k), (T["SO%d" % k][:], "SO%d" % k),
                                    (T["S%d" % k][:], "S%d" % k))):
            mm(out, T[ws[i]][:], x, i == 0, False, [ws[i], r], [nm])

    def apart(t):
        k = t - 1
        for a in range(EV, 8):
            act(T.EA[:, a, 0:128 - 16 * a], T.PB[:, 128 * k + 16 * a:128 * k + 128], Act.Abs, ["PB%d" % k, "PF%d" % k], ["EA%d" % a],
                bias=T.PF[:, 8 * k + a:8 * k + a + 1], scale=-1.0)

    def asked(t, a, last):
        k = t - 1
        if a < EV:
            ts(T.E[:, a, 0:128 - 16 * a], T.PB[:, 128 * k + 16 * a:128 * k + 128], T.PF[:, 8 * k + a:8 * k + a + 1],
               T["FN%d" % t][:, a:a + 1], Op.is_equal, Op.mult, ["PB%d" % k, "PF%d" % k, "FN%d" % t], ["E%d" % a])
        else:
            act(T.E[:, a, 0:128 - 16 * a], T.EA[:, a, 0:128 - 16 * a], Act.Relu, ["EA%d" % a, "FN%d" % t], ["E%d" % a],
                bias=T["FN%d" % t][:, a:a + 1], scale=-1.0)
        if a < 7:
            mm(T.pD[:, 16 * a + 16:128], T.BLK[:], T.E[:, a, 16:128 - 16 * a], False, False, ["BLK", "E%d" % a], ["pD"])
        if a in (EV - 1, 7):
            b0, b1 = (EV, 8) if a == 7 else (0, EV)
            mm(T.pD[:, 16 * b0:16 * b1], T.TRI[:], T.E[:, b0:b1, 0:16], False, last, ["TRI"] + ["E%d" % b for b in range(b0, b1)], ["pD"])

    for k in range(5):
        weights[k]()
        blocks("S0", [k], "v")
    blocks("S0", range(5, 8), "s")
    send(prv, "WN", T.WH[:], ["WH"])
    repeat(0, 0)
    addend(0)
    repeat(0, 1)
    for nm in EIGHTS:
        begin(nm)
    for nm in EIGHTS:
        linear(nm, "WH", nm == "pX")
    addend(1)
    ms(T.NUM[:, W:TW], 4094.0, ["NUMx"])
    for nm in ("pF", "pY"):
        whole_part(nm)
    test_constants()
    for nm in ("pF", "pY"):
        remainder(nm)
        offsets(nm, 0)
    for k in range(len(PACKS)):
        pack(k)
    scaled("BN", "BP", -1.0)
    scaled("KQ", "KB", 1.0 / 32, slice(0, 32))

    for t in range(ST):
        s_, St = "S%d" % t, T["S%d" % t]
        tests(t, [lambda: effects(t, 0)])
        if t == ST - 1:
            dma("y", T.yp[:, 0:512], T.YP[0:128:16, 0:512], ["YP%d" % k for k in range(4)], [], "d_yp0")
        if 1 <= t <= 3:
            open_sums(t)
        first_hit(t)
        if t < ST - 1:
            for nm in ("pX", "pY", "pF"):
                begin(nm)
        later = place(t) if t < ST - 1 else []

        def fill():
            if later:
                later.pop(0)()

        ki, kn = T.KI[:], "KI"
        fill()
        ts(T.CI[:, 0:8], ki, 4095, None, Op.bitwise_and, None, [kn], ["CI"])
        if 1 <= t <= 3:
            tt(T.FA[:, t - 1], ki, T.THR[:], Op.is_lt, [kn, "THR"], ["FA%d" % t])
            send(prv, "FN%d" % t, T.FA[:, t - 1], ["FA%d" % t])
        else:
            fill()
        col = T.CU[:, 0:8]
        if t == ST - 1:
            ts(T.CI[:, 8:16], ki, 12, 63, Op.arith_shift_right, Op.bitwise_and, [kn], ["KK"])
            cp(T.CU[:], T.CI[:], ["CI", "KK"], ["CU"])
            tt(T.YS[:], T.EF[:, 0:TW].indirect(col), St[:], Op.add, EFr + ["CU", s_], ["YS"])
            dma("y", T.ys[:], T.YS[:], ["YS"], [], "d_ys")
            numbers(t, T.CU[:, 8:16])
            dma("s", T.yp[:, 512:640], T.YP[0:128:16, 512:640], ["YP4"], [], "d_yp1")
            break
        cp(col, T.CI[:, 0:8], ["CI"], ["CU"])
        fill()
        so, So, Gt = "SO%d" % t, T["SO%d" % t], T["G%d" % t][:]
        tt(So[:], T.EF[:, 0:TW].indirect(col), St[:], Op.add, EFr + ["CU", s_], [so])
        act(Gt, T.A[:, 0:TW].indirect(col), Act.Copy, At + ["CU"], ["G%d" % t])
        if t == 0:
            send(nxt, "S1", So[:], [so])
        else:
            send(prv, "GN%d" % t, Gt, ["G%d" % t])
            send_together([(nxt, "S%d" % (t + 1), So, [so], 1), (prv, "SN%d" % t, So, [so], 1)])
        gn, ga = "GN%d" % t, "G%d" % (t - 1)
        left = [list(range(EV)), list(range(EV, 8))]

        def compare(i):
            a = left[i].pop(0)
            asked(t, a, not left[0] + left[1])

        forward = dict(
            masks_s=lambda: blocks(so, range(0, NS_), "s"), masks_v=lambda: blocks(so, range(NS_, NG), "v"),
            repeat0=lambda: repeat(t + 1, 0), repeat1=lambda: repeat(t + 1, 1), addend=lambda: addend(0),
            addend1=lambda: addend(1),
            probes=lambda: linear("pX", "WN", True),
            again_a=lambda: linear("pF", "WN", False), again_b=lambda: linear("pY", "WN", False),
            whole_a=lambda: whole_part("pF"), whole_b=lambda: whole_part("pY"),
            rest_a=lambda: remainder("pF"), rest_b=lambda: remainder("pY"),
            offsets_a=lambda: offsets("pF", t + 1), offsets_b=lambda: offsets("pY", t + 1),
            fill=fill, kept=lambda: kept(t) if t <= 2 else None)
        back = dict(
            w_open=lambda: open_sum(t, "pE", T.pE[:, 256:384], ["N4", "ID", "IS", "NS"]),
            apart=lambda: apart(t),
            e=lambda: compare(0), es=lambda: compare(1),
            lows=lambda: act(T.NB[:], T[gn][:], Act.Identity, [gn], ["NB"], bias=1280.0),
            w_bounds=lambda: mm(T.pE[:, 256:384], T.I4[:], T[gn][:], False, False, ["I4", gn], ["pE"]),
            u_lows=lambda: mm(T.pU[:, 0:128], T.ID[:], T.NB[:], False, True, ["ID", "NB"], ["pU"]),
            w_lows=lambda: mm(T.pE[:, 256:384], T.NI[:], T.NB[:], False, True, ["NI", "NB"], ["pE"]),
            u=lambda: tt(T.U[:], T.pU[:, 0:128], T[ga][:], Op.min, ["pU", ga], ["U"]),
            w=lambda: act(T.UW[:], T.pE[:, 256:384], Act.Relu, ["pE"], ["UW"]),
            lowest=lambda: scan(T.ZD[:], T.RSD[:], T.pD[:, 0:128], 0.0, Op.max, Op.min, ["RSD", "pD"], ["ZD"]),
            served=lambda: cp(T.OU[:], T.ZD[:, 15:128:16], ["ZD"], ["OU"]),
            scatter=lambda: tt(T.A[:, 0:TW].indirect(T.OU[:, 0:8]), T.U[:], T.UW[:], Op.add, ["U", "UW", "OU"], At))
        for name in ORDER.split("|")[0 if near(nxt) else 1].split():
            if name in forward:
                forward[name]()
            elif t >= 1:
                back[name]()
        while later:
            fill()

    wait("g", list(total.items()))
